import numpy as np, ml_dtypes
CORES = [48,51,52,55]
N = 4
BF = ml_dtypes.bfloat16
def gentries(a):
    return np.ascontiguousarray(a.reshape(8, 16, -1).transpose(0, 2, 1)).reshape(8, -1)
def gtable(e):
    e = np.asarray(e); return np.ascontiguousarray(e.reshape(8, -1, 16).transpose(0, 2, 1)).reshape(128, -1).astype(np.int32)
B, J, CAP, RO, Q = 3328, 4096, 64, 3, 4096
LN, LJ = 2, 12
M = N * CAP; W = B + RO * M
WT = (14 * np.arange(16) + 9)[:, None]
def decode(n):
    C = np.add.accumulate((n * n[..., ::-1]) >> 12, axis=-1)
    x = (C[..., -1:] * np.arange(J)) >> LJ
    return np.add.reduce((C[..., None] <= x[..., None, :]).astype(np.int64), axis=-2)
def combine(x, y, z):
    q = x.shape[-1] // 4
    k = np.concatenate([np.minimum(x[..., :q], y[..., :q]), np.maximum(x[..., q:2 * q], y[..., q:2 * q]), np.abs(x[..., 2 * q:3 * q] - y[..., 2 * q:3 * q]), x[..., 3 * q:] + y[..., 3 * q:]], axis=-1)
    return np.minimum(k, z)
def sizes(c):
    c = np.sort(c, axis=-1); z = np.zeros(c.shape[:-1] + (1,), np.int64)
    return np.diff(np.concatenate([z, c, z + B - 256], axis=-1), axis=-1) + 64
def span(rng, v, share):
    o = rng.integers(0, B, (3, N, 8, 1, 2048)); x, y, z = [np.take_along_axis(v, i, 3) for i in o]
    s = np.sort(np.add.reduce(combine(x, y, z), axis=2), axis=-1)
    m = np.minimum(np.maximum((2048 * share).astype(np.int64), 1), 2048); k = (rng.random((N, 8)) * (2048 - m)).astype(np.int64)
    return np.concatenate([np.take_along_axis(s, k[..., None], 2), np.take_along_axis(s, (k + m - 1)[..., None], 2)], axis=2)
def shares(rng):
    return CAP * N * 2.0 ** -LJ * rng.choice(np.array([0.4, 0.8, 1.0, 1.5]), (N, 8))
def parts(rng):
    e = rng.choice(np.array([0.5, 1.0, 1.0, 2.0]), (N, 8, 16, 1))
    v = np.minimum((256 * rng.random((N, 8, 16, B)) ** e).astype(np.int64), 255)
    n = sizes(rng.integers(0, B - 255, (N, 8, 3))); r = rng.integers(0, 4096, (3, N, 8, RO, J))
    u = (rng.random((N, 8, Q)) < rng.choice(np.array([0.05, 0.2, 0.5]), (N, 8, 1))).astype(np.int64)
    return v, n, span(rng, v, shares(rng)), r, u
def pack(v, n, lim, r, u):
    t = [np.stack([gtable(a.reshape(8, -1)) for a in b]) for b in r]
    return {"bank": np.ascontiguousarray(v.reshape(N, 128, B)).astype(np.float32).astype(BF), "ncl": n.astype(np.int32), "lim": lim.astype(np.int32),
            "ra": t[0], "rb": t[1], "rc": t[2], "used": u.astype(np.int32)}
def goals(rng, k):
    return np.stack([rng.permutation(Q - 1)[:k] + 1 for p in range(N)]) * N + np.arange(N)[:, None]
def keyed(rng, d):
    c = rng.integers(1, 256, (16, d.size)); c[[0, 1, 15]] = rng.integers(40, 101, (3, d.size))
    e = (d - np.add.reduce(c * WT, axis=0)) & (N * Q - 1)
    c[15] += e // 219; e = e % 219; c[0] += e // 9 - 5 * (e % 9); c[1] += 2 * (e % 9)
    return c
def put(rng, v, n, q, g, d):
    s = np.add.accumulate(n[q, g]) - n[q, g]; v[q, g][:, s] = 255; v[q, g][:, s + 1] = 0
    w = rng.permutation(np.setdiff1d(np.arange(B), np.concatenate([s, s + 1])))[:d.size]
    v[q, g][:, w] = keyed(rng, d.reshape(-1)); return w.reshape(d.shape)
def deal(rng, col, at, w):
    o = rng.permutation(np.repeat(np.arange(N), CAP)); at = np.sort(rng.permutation(at)[:M])
    for p in range(N): col[at[o == p]] = w[p]
def play(r, n, q, g, t, col):
    h = J // 4; k = B + t * M; r[:2, q, g, t] = 0; r[2, q, g, t] = (col * 4096 + k - 1) // k
    if t == 0:
        m = n[q, g][3 - decode(n[q, g])[2 * h:3 * h]]; r[1, q, g, 0, 2 * h:3 * h] = (4096 + m - 1) // m
def setup_inputs(rng):
    return pack(*parts(rng))
def setup_inputs_room(rng):
    v, n, lim, r, u = parts(rng); lim[:] = (1500, 2600)
    for q in range(N):
        for g in range(8):
            m = n[q, g]; p = np.concatenate([np.arange(k) for k in m]); live = p >= np.repeat(m // 2, m)
            c = np.where(live, rng.integers(110, 150, (16, B)), rng.integers(0, 90, (16, B)))
            c[0] += (p - np.add.reduce(c * WT, axis=0)) & (N - 1)
            c[:, p == 0] = 0; c[:, p == 1] = 255; v[q, g] = c
            t = rng.choice(np.array([0, 1, CAP - 1, CAP, CAP + 1, 2 * CAP]), N)
            if q == 0: t[1] = (CAP, CAP + 1, CAP - 1, CAP, 0, 1, 2 * CAP, CAP)[g]
            if g == 6: t[2] = 0
            own = np.full(J, -1); own[rng.permutation(J)[:int(np.sum(t))]] = rng.permutation(np.repeat(np.arange(N), t))
            a = decode(m); na = m[a]; nb = m[3 - a]; h = na // 2
            dead = 2 + (rng.random(J) * (h - 2)).astype(np.int64)
            good = h + (own - h) % N + N * (rng.random(J) * ((na - h - N) // N + 1)).astype(np.int64)
            i = np.where(own < 0, dead, good); y = (np.arange(J) < J // 4).astype(np.int64)
            r[0, q, g, 0] = (i * 4096 + na - 1) // na; r[1, q, g, 0] = (y * 4096 + nb - 1) // nb; r[2, q, g, 0] = (4096 + B - 1) // B
    return pack(v, n, lim, r, u)
def setup_inputs_ends(rng):
    v, n, lim, r, u = parts(rng); v[..., 0] = 0; v[..., B - 1] = 255
    for g in range(4):
        n[:, g] = 64; n[:, g, g] = B - 192
    n[:, 5] = n[:, 2]; lim[0, 5] = (1, 4080)
    for g in (0, 2, 4): r[:, :, g] = rng.choice(np.array([0, 1, 4094, 4095]), (3, N, RO, J))
    lim[:, 0] = (0, 4080); lim[:, 2] = (4080, 4080); lim[:, 4] = (0, 0); lim[:, 6, 0] = lim[:, 6, 1]
    r[:, :, 2, 0, J - 1] = 4095; r[2, :, 4, 0, :8] = 0; u[:, 2] = 0; u[:, 4] = 0
    r[2, :, 0, 0, :8] = 0; u[:, 0] = 0
    lim[:, 1] = (1, 4080); lim[:, 3] = (1, 4080); lim[:, 7] = (0, 4079); u[:, 1] = 0; u[:, 3] = 0; u[:, 7] = 0
    full = goals(rng, RO * M).reshape(N, RO, N, CAP)
    grid = goals(rng, M).reshape(N, N, CAP); grid[1:, N - 1, CAP - 1] = grid[1:, 0, 0]
    many = goals(rng, 2 * CAP); at = np.concatenate([np.arange(J // 4, J // 2), np.arange(3 * J // 4, J)])
    for q in range(N):
        w = put(rng, v, n, q, 3, full[:, :, q])
        for t in range(RO):
            col = np.full(J, 1); deal(rng, col, at, w[:, t]); play(r, n, q, 3, t, col)
        i = J // 8 + rng.permutation(J // 8)[:4]; r[0, q, 3, RO - 1, i] = rng.integers(1000, 4096, 4); r[2, q, 3, RO - 1, i] = 0
        w = put(rng, v, n, q, 7, grid[:, q])
        if q == N - 1: w[0, CAP - 1] = 1
        col = np.zeros(J, np.int64); deal(rng, col, np.arange(J), w); play(r, n, q, 7, 0, col)
        w = put(rng, v, n, q, 1, many[(q + 1) % N]); col = np.full(J, 1); k = J // 4
        if q > 0: k += int(rng.integers(0, CAP))
        i = np.sort(rng.permutation(J // 2)[:k]); col[i] = w[rng.integers(0, CAP, k)]; col[i[:CAP]] = w[:CAP]
        col[J // 2 + rng.permutation(J // 2)[:2 * CAP]] = np.tile(w[CAP:], 2); play(r, n, q, 1, 0, col)
    return pack(v, n, lim, r, u)
def setup_inputs_alike(rng):
    v, n, lim, r, u = parts(rng)
    a = rng.integers(1, 255, (8, 16, 3)); tw = np.zeros((16, 1), np.int64); tw[:4, 0] = (1, -1, -1, 1)
    pool = np.concatenate([a, a + tw], axis=2)
    for g in range(1, 8, 2):
        v[:, g] = pool[g][:, rng.integers(0, 6, (N, B))].transpose(1, 0, 2)
        for q in range(N):
            e = np.add.accumulate(n[q, g]); v[q, g][:, e - n[q, g]] = pool[g][:, :1]; v[q, g][:, e - 1] = pool[g][:, 3:4]
    lim[:, 1::2] = (0, 4080); u[:, 1::2] = 0; r[:, :, 1::2, 0, 0] = 0; r[:, :, 1::2, 0, 1] = 4095
    v[:, 2] = v[0, 2]; n[:, 2] = n[0, 2]; lim[:, 2] = lim[0, 2]; r[:, :, 2] = r[:, :1, 2]
    return pack(v, n, lim, r, u)
def setup_inputs_cold(rng):
    v, n, lim, r, u = parts(rng); o = rng.permutation(N); g = int(rng.integers(0, 8))
    lim[o[0]] = (1, 0); lim[o[0], 1::2] = (1600, 1000); lim[o[1]] = (0, 4080)
    lim[:, g] = (1700, 1100); lim[o[0], g] = (2000, 1999); lim[o[1], g] = (4080, 0); u[:, (g + 1) % 8] = 1; u[:, (g + 2) % 8] = 0
    u[o[2], (g + 3) % 8] = 1
    return pack(v, n, lim, r, u)
def setup_inputs_spread(rng):
    v, n, lim, r, u = parts(rng)
    v = np.minimum((np.exp2(8 * rng.random((N, 8, 1, B))) * rng.random((N, 8, 16, B))).astype(np.int64), 255)
    n = sizes(((B - 256) * rng.random((N, 8, 3)) ** 4).astype(np.int64))
    e = rng.choice(np.array([0.5, 1.0, 2.0, 3.0]), (3, N, 8, RO, 1)); r = np.minimum((4096 * rng.random((3, N, 8, RO, J)) ** e).astype(np.int64), 4095)
    u = (rng.random((N, 8, Q)) < 0.8 * rng.random((N, 8, 1))).astype(np.int64)
    return pack(v, n, span(rng, v, shares(rng)), r, u)
def check_inputs(d):
    bad = []; b = np.asarray(d["bank"]).astype(np.float32)
    if not np.all((b >= 0) & (b <= 255) & (b == np.floor(b))): bad.append("bank: whole numbers from 0 to 255")
    for k, lo, hi in (("ncl", 64, B), ("lim", 0, 4080), ("ra", 0, 4095), ("rb", 0, 4095), ("rc", 0, 4095), ("used", 0, 1)):
        if np.min(d[k]) < lo or np.max(d[k]) > hi: bad.append("range of " + k)
    if np.any(np.sum(np.asarray(d["ncl"]).astype(np.int64), axis=-1) != B): bad.append("sums of ncl")
    return bad
def reference(bank, ncl, lim, ra, rb, rc, used):
    v = np.zeros((N, 8, 16, W), np.int32); v[..., :B] = bank.astype(np.float32).astype(np.int32).reshape(N, 8, 16, B)
    n = np.zeros((N, 8, 4 + RO), np.int64); n[:, :, :4] = ncl
    la, lb, lc = [np.stack([gentries(a) for a in b]).astype(np.int64).reshape(N, 8, RO, J) for b in (ra, rb, rc)]
    free = used == 0; lo = lim[:, :, :1]; hi = lim[:, :, 1:]; take = np.take_along_axis
    for t in range(RO):
        s = 4 + t; m = n[:, :, :s].copy(); start = np.add.accumulate(m, axis=2) - m; tot = np.add.reduce(m, axis=2)
        a = decode(m); b = s - 1 - a
        ix = take(start, a, 2) + ((take(m, a, 2) * la[:, :, t]) >> 12)
        iy = take(start, b, 2) + ((take(m, b, 2) * lb[:, :, t]) >> 12)
        iz = (tot[:, :, None] * lc[:, :, t]) >> 12
        x, y, z = [take(v, i[:, :, None, :], 3) for i in (ix, iy, iz)]
        k = combine(x, y, z)
        total = np.add.reduce(k, axis=2); key = np.add.reduce(k * WT, axis=2)
        alive = (total >= lo) & (total <= hi); owner = key & (N - 1); bucket = (key >> LN) & (Q - 1)
        for p in range(N):
            for g in range(8):
                got = [np.flatnonzero(alive[q, g] & (owner[q, g] == p))[:CAP] for q in range(N)]
                c = np.concatenate([k[q, g][:, got[q]] for q in range(N)], axis=1); bu = np.concatenate([bucket[q, g, got[q]] for q in range(N)])
                first = np.sort(np.unique(bu, return_index=True)[1])
                keep = first[free[p, g, bu[first]]]; e = int(tot[p, g])
                v[p, g][:, e:e + len(keep)] = c[:, keep]; free[p, g, bu[keep]] = False; n[p, g, s] = len(keep)
    return {"y": np.ascontiguousarray(v[..., B:]).reshape(N, 128, RO * M).astype(np.float32).astype(BF)}

@@ -1,0 +1,474 @@
+import numpy as np
+from concourse.bass import DstId, RemoteDMATransfer
+from concourse.mybir import dt, AluOpType as A, AxisListType, ActivationFunctionType as F
+
+B, J, CAP, RO, Q, N = 3328, 4096, 64, 3, 4096, 4
+TR = 4096
+DUM = 288
+M23 = 8388608.0
+M27 = 201326592.0
+EPS = 2.0 ** -13
+
+SCRATCH = {}
+
+
+def _sb(dtype, **kw):
+    for n, w in kw.items():
+        SCRATCH[n] = ("sbuf", [128, w], dtype)
+
+
+_sb("bfloat16", BANK=TR + 256, CAND=J + DUM, TX=J, TY=J, TZ=J, USED=TR + 256, ONE256=256, FM=1024, SC=1024, I1=256, I2=256, I3=256,
+    UG=256, E=4096, XP=256, XS=256, SK=16, SEND0=256, SEND1=256, SEND2=256, LAND0=256, LAND1=256, LAND2=256, BO=128, BO16=128,
+    BO256=128, NBO=128, IDN=128, NID=128, UP=128, NU=128, SU=128, WB=128, LS=2048, WK4=2048, WKF=2048, KP=256, MK2=256, RST=256,
+    rowg=128, rowl=128, rowk=128, rowh=128, R256=256, sB=64, IOC=258, JLC=128, AL=258, GM=128, LT=1024, EL=128)
+_sb("float32", sR=256, IC0=258, IC1=258, cols=64, RN=8, ra8=8, AS=8, M0=8, M1=8, AA=8, AB=8, T8=8, PRE=16, HL=16, DD=16, I16=16, TB=16,
+    TI=16, NK=16, C16=16, C256=16, W1T=64, W2S=72, W3S=1040, PK1=256, PK2=256, PK3=256, SEL8=128, NF=8, lims=8, TRI=128, TRIS=128,
+    ONE=128, ONES=128, rk6=128, F1=128, F2=128, ZT=256, XT=256, YT=256, AB1=256, DE=256, BC=16, NV=16, PO=16)
+_sb("int32", RA=768, RB=768, RC=768, ip=8, NI=8, WI=4, KI=256, OW=256, KRI=256, BRI=256, KBI=16, BBI=16)
+_sb("uint16", XO=256, YO=256, ZO=256, O1=16, O2=16, O3=16, UO=16, SO=16, UO2=16, BR=256)
+SCRATCH["UD"] = ("dram", [8, 4096], "bfloat16")
+for _b in range(8):
+    SCRATCH["P%d" % _b] = ("psum", [128, 512], "float32")
+
+SEMAPHORES = ["cV", "cS", "cP", "cG"] + ["d%d" % i for i in range(12)] + ["arr0", "arr1", "arr2", "snt0", "snt1", "snt2"]
+
+
+def rank_program(g, core, T, topo):
+    rank = T.rank_of(core)
+    if rank is None:
+        return
+    queue = {"V": g.vector, "S": g.scalar, "P": g.tensor, "G": g, "Y": g.sync}
+    count, snap, recs, names, nd = {}, {}, {}, {}, [0]
+    known = {q: {} for q in queue}
+
+    def psum(b):
+        return b[0] == "P" and b[1:].isdigit()
+
+    def deps(q, reads, writes):
+        need = {}
+        for lst, w in ((reads, False), (writes, True)):
+            for b, lo, hi in lst:
+                for r in recs.get(b, []):
+                    if psum(b):
+                        if r[4] == q and (q == "P" or r[0] >= hi or r[1] <= lo or not (w or r[2])):
+                            continue
+                    elif r[0] >= hi or r[1] <= lo or not (w or r[2]):
+                        continue
+                    need[r[3][0]] = max(need.get(r[3][0], 0), r[3][1])
+        for s, v in need.items():
+            if known[q].get(s, 0) < v:
+                queue[q].wait_ge(T.sem[s], v)
+                known[q][s] = v
+        for s, v in need.items():
+            for s2, v2 in snap.get((s, v), {}).items():
+                known[q][s2] = max(known[q].get(s2, 0), v2)
+
+    def note(q, reads, writes, tok, remote=False):
+        snap[tok] = {} if remote else dict(known[q])
+        for b, lo, hi in writes:
+            recs[b] = [r for r in recs.get(b, []) if not (r[0] >= lo and r[1] <= hi)] + [(lo, hi, True, tok, q)]
+        for b, lo, hi in reads:
+            keep = [r for r in recs.get(b, []) if r[2] or r[4] != q or not (r[0] >= lo and r[1] <= hi)]
+            recs[b] = keep + [(lo, hi, False, tok, q)]
+
+    def do(q, fn, reads, writes):
+        deps(q, reads, writes)
+        s = "c" + q
+        count[s] = count.get(s, 0) + 1
+        fn().then_inc(T.sem[s], 1)
+        note(q, reads, writes, (s, count[s]))
+
+    def mm(lst):
+        reads = [x[3] for x in lst] + [x[4][:3] for x in lst]
+        writes = [x[:3] for x in lst]
+        deps("P", reads, writes)
+        last = None
+        for o, c0, c1, lh, rh, st, sp in lst:
+            kp = rh[4] if len(rh) > 4 else 128
+            step = rh[3] if len(rh) > 3 else 1
+            last = g.tensor.matmul(T[o][:, c0:c1], T[lh[0]][0:kp, lh[1]:lh[2]], T[rh[0]][0:kp, rh[1]:rh[2]:step], st, sp)
+        count["cP"] = count.get("cP", 0) + 1
+        last.then_inc(T.sem["cP"], 1)
+        note("P", reads, writes, ("cP", count["cP"]))
+
+    def dma(q, out, in_, reads, writes, sem=None):
+        deps(q, reads, writes)
+        if sem is None:
+            sem = "d%d" % nd[0]
+            nd[0] += 1
+        queue[q].dma_start(out, in_).then_inc(T.sem[sem], 16)
+        count[sem] = count.get(sem, 0) + 16
+        note(q, reads, writes, (sem, count[sem]))
+
+    def ap(r):
+        return T[r[0]][:, r[1]:r[2]:r[3]] if len(r) > 3 else T[r[0]][:, r[1]:r[2]]
+
+    def pair(x):
+        return isinstance(x, tuple) and isinstance(x[0], tuple)
+
+    def regs(*xs):
+        out = []
+        for x in xs:
+            if pair(x):
+                out += [x[0][:3], x[1][:3]]
+            elif isinstance(x, tuple):
+                out.append(x[:3])
+        return out
+
+    def view(x):
+        return ap(x[0]).indirect(ap(x[1])) if pair(x) else ap(x) if isinstance(x, tuple) else x
+
+    def ts(out, in0, s1, op0, s2=None, op1=None):
+        if op1 is None:
+            do("V", lambda: g.vector.tensor_scalar(ap(out), view(in0), view(s1), None, op0), regs(in0, s1), regs(out))
+        else:
+            do("V", lambda: g.vector.tensor_scalar(ap(out), view(in0), view(s1), view(s2), op0, op1), regs(in0, s1, s2), regs(out))
+
+    def tt(out, in0, in1, op):
+        do("V", lambda: g.vector.tensor_tensor(ap(out), view(in0), view(in1), op), regs(in0, in1), regs(out))
+
+    def cp(out, in0):
+        if pair(out):
+            do("V", lambda: g.vector.tensor_copy(view(out), ap(in0)), regs(in0) + [out[1][:3]], [out[0][:3]])
+        else:
+            do("V", lambda: g.vector.tensor_copy(ap(out), view(in0)), regs(in0), regs(out))
+
+    def scan(out, d0, d1, init, op0, op1):
+        do("V", lambda: g.vector.tensor_tensor_scan(ap(out), ap(d0), ap(d1), view(init), op0, op1), regs(d0, d1, init), regs(out))
+
+    def red(out, in0):
+        do("V", lambda: g.vector.tensor_reduce(ap(out), ap(in0), AxisListType.X, A.add), regs(in0), regs(out))
+
+    def fill(r, c):
+        do("V", lambda: g.vector.memset(ap(r), c), [], regs(r))
+
+    def act(out, in0, func, scale=1.0, bias=0.0):
+        do("S", lambda: g.scalar.activation(ap(out), view(in0), func, bias=view(bias), scale=view(scale)), regs(in0, scale, bias), regs(out))
+
+    def iota(r, pattern, cm=0):
+        if SCRATCH[r[0]][2] == "int32":
+            do("G", lambda: g.iota(ap(r), pattern, 0, cm), [], regs(r))
+        else:
+            do("G", lambda: g.iota(ap(r), pattern, 0, cm, allow_small_or_imprecise_dtypes=True), [], regs(r))
+
+    def R(b, lo=0, hi=None, *step):
+        return (b, lo, SCRATCH[b][1][1] if hi is None else hi) + step
+
+    def C(name):
+        if name not in names:
+            names[name] = len(names)
+        return ("cols", names[name], names[name] + 1)
+
+    def lists_z(t):
+        if t:
+            ts(C("Tq"), C("Told"), C("e%d" % t), A.add, 2.0 ** -12, A.mult)
+        ts(R("ZT"), R("RC", 256 * t, 256 * t + 256), C("Tq") if t else B / 4096.0, A.mult, -1920.5 + EPS, A.add)
+        ts(R("ZO"), R("ZT"), M23 + 1920.0, A.add, M23, A.subtract)
+
+    dma("Y", T.NI[0:8, 0:4], T.ncl[:, :], [], [("NI", 0, 4)])
+    dma("S", T.NI[0:8, 4:6], T.lim[:, :], [], [("NI", 4, 6)])
+    dma("Y", T.RC[:, 0:768], T.rc[:, :], [], [R("RC")])
+    dma("S", T.BANK[:, 0:B], T.bank[:, :], [], [("BANK", 0, B)])
+    dma("Y", T.RA[:, 0:768], T.ra[:, :], [], [R("RA")])
+    dma("Y", T.RB[:, 0:768], T.rb[:, :], [], [R("RB")])
+    dma("Y", T.KRI[:, 0:256], T.used[:, :], [], [R("KRI")])
+
+    ip = ("ip", 0, 1)
+    iota(ip, [[0, 1]], 1)
+    for b, pat in (("SEL8", [[1, 8], [0, 16]]), ("rowg", [[1, 8], [0, 16]]), ("ra8", [[1, 8]]), ("rowk", [[0, 16], [1, 8]]), ("rowl", [[0, 8], [1, 16]]),
+                   ("rowh", [[0, 8], [1, 2], [0, 8]])):
+        iota(R(b), pat)
+    iota(R("IC0", 0, 257), [[1, 257]])
+    for b, pat in (("R256", [[0, 16], [1, 16]]), ("sB", [[1, 64]]), ("sR", [[0, 4], [1, 64]]), ("I16", [[16, 16]]), ("C16", [[16, 4], [0, 4]]),
+                   ("C256", [[256, 4], [0, 4]])):
+        iota(R(b), pat)
+    fill(R("BANK", B, TR + 256), 0.0)
+    fill(R("RN"), 0.0)
+    ts(("ip", 1, 2), ip, 15, A.bitwise_and)
+    ts(("ip", 2, 3), ip, 7, A.bitwise_and)
+    ts(("ip", 3, 4), ip, 3, A.logical_shift_right, 1, A.bitwise_and)
+    ts(("ip", 4, 5), ip, 4, A.logical_shift_right)
+    ts(("ip", 5, 6), ip, 1, A.bitwise_and)
+    for i, c in enumerate("plkhg"):
+        cp(C(c), ("ip", i, i + 1))
+    ts(R("SEL8"), R("SEL8"), C("p"), A.is_equal)
+    ts(R("BO"), R("rowg"), C("g"), A.is_equal)
+    ts(C("km1"), C("k"), -1.0, A.add)
+    ts(C("k6"), C("k"), 6.0, A.is_ge, 100.0, A.mult)
+    tt(C("kk"), C("k"), C("k6"), A.add)
+    ts(C("m0"), C("k"), 0.0, A.is_equal)
+    ts(C("m1"), C("k"), 1.0, A.is_equal)
+    tt(C("m01"), C("m0"), C("m1"), A.subtract)
+    ts(C("h0"), C("h"), -1.0, A.mult, 1.0, A.add)
+    ts(C("h0a"), C("h0"), 4096.0, A.mult)
+    ts(C("h0b"), C("h0"), 16.0, A.mult)
+    ts(C("sg16"), C("h"), 0.125, A.mult, -0.0625, A.add)
+    ts(C("k7h"), C("k"), 7.0, A.is_equal, C("h0"), A.mult)
+    ts(C("k6h"), C("k"), 6.0, A.is_equal, C("h0"), A.mult)
+    ts(C("chi"), C("k7h"), -1920.0, A.mult)
+    ts(C("clo"), C("k6h"), EPS, A.mult)
+    ts(C("k7m"), C("k7h"), -0.5, A.mult)
+    tt(C("clo"), C("clo"), C("k7m"), A.add)
+    for t in range(RO):
+        ts(C("ml%d" % t), C("k"), float(3 + t), A.is_equal)
+    ts(R("M0"), R("ra8"), C("k"), A.is_equal)
+    ts(R("M1"), R("ra8"), C("km1"), A.is_equal)
+    ts(R("AS"), R("ra8"), C("kk"), A.add)
+    ts(R("rk6"), R("rowk"), 6.0, A.is_ge, -100.0, A.mult)
+    tt(R("rk6"), R("rk6"), R("rowk"), A.add)
+    ts(R("F1"), R("rk6"), C("k"), A.is_gt, C("h0a"), A.mult)
+    tt(R("TRI"), R("F1"), R("BO"), A.mult)
+    ts(R("ONE"), R("BO"), C("h0b"), A.mult)
+    ts(R("F2"), R("rowh"), 2.0, A.mult, -1.0, A.add)
+    tt(R("TRIS"), R("TRI"), R("F2"), A.mult)
+    tt(R("ONES"), R("ONE"), R("F2"), A.mult)
+    ts(R("IC0", 0, 257), R("IC0", 0, 257), C("h"), A.add)
+    ts(R("IC1", 0, 257), R("IC0", 0, 257), 257.0, A.is_equal, -257.0, A.mult)
+    tt(R("IOC", 0, 257), R("IC0", 0, 257), R("IC1", 0, 257), A.add)
+    ts(R("F1"), R("rowl"), C("sg16"), A.mult)
+    tt(R("F1"), R("F1"), R("BO"), A.mult)
+    ts(R("F2"), R("BO"), 1024.0, A.mult, -1024.0, A.add)
+    tt(R("JLC"), R("F1"), R("F2"), A.add)
+    do("V", lambda: g.vector.tensor_copy(T.NF[0:8, 0:6], T.NI[0:8, 0:6]), [("NI", 0, 6)], [("NF", 0, 6)])
+    mm([("P0", 8, 14, ("SEL8", 0, 128), ("NF", 0, 6, 1, 8), True, True)])
+    lists_z(0)
+    cp(("RN", 0, 3), ("P0", 8, 11))
+    cp(C("e0"), ("P0", 11, 12))
+    cp(("lims", 0, 2), ("P0", 12, 14))
+    ts(C("Told"), C("e0"), -1.0, A.mult, float(B), A.add)
+
+    def prepare(t):
+        s = 4 + t
+        ts(R("AA"), R("AS"), float(s - 1), A.is_equal)
+        ts(R("AB"), R("AS"), float(s), A.is_equal)
+        for m, c in (("M0", "PNL"), ("AA", "PNR"), ("M1", "dS"), ("AB", "Qc")):
+            tt(R("T8"), R("RN"), R(m), A.mult)
+            red(C(c), R("T8"))
+        tt(("PRE", 0, 1), C("PNL"), C("dS"), A.subtract)
+        tt(("PRE", 1, 2), C("PNR"), C("Qc"), A.subtract)
+        ts(C("dSb"), C("m0"), C("Told"), A.mult, C("PNR"), A.subtract)
+        for c, i in (("dS", 2), ("dSb", 6)):
+            ts(("HL", i, i + 1), C(c), M27, A.add, M27, A.subtract)
+            tt(("HL", i + 1, i + 2), C(c), ("HL", i, i + 1), A.subtract)
+            tt(("HL", i, i + 1), ("HL", i, i + 1), C("chi"), A.add)
+            tt(("HL", i + 1, i + 2), ("HL", i + 1, i + 2), C("clo"), A.add)
+
+    def decode_xy(t):
+        e = C("e%d" % t)
+        ts(C("NL"), C("ml%d" % t), e, A.mult, C("PNL"), A.add)
+        ts(C("NR"), C("m0"), e, A.mult, C("PNR"), A.add)
+        tt(("WI", 0, 1), C("NL"), C("NR"), A.mult)
+        ts(("WI", 1, 2), ("WI", 0, 1), 12, A.arith_shift_right)
+        cp(C("w"), ("WI", 1, 2))
+        mm([("P0", 0, 1, R("TRI"), C("w"), True, True), ("P0", 1, 2, R("ONE"), C("w"), True, True)])
+        mm([("P7", 0, 1, R("TRIS"), C("w"), True, True), ("P7", 1, 2, R("ONES"), C("w"), True, True)])
+        ts(("DD", 0, 1), C("ml%d" % t), e, A.mult, ("PRE", 0, 1), A.add)
+        ts(("DD", 1, 2), C("m01"), e, A.mult, ("PRE", 1, 2), A.add)
+        ts(("DD", 2, 4), ("DD", 0, 2), M27, A.add, M27, A.subtract)
+        tt(("DD", 4, 6), ("DD", 0, 2), ("DD", 2, 4), A.subtract)
+        ts(R("AL", 0, 257), R("IOC", 0, 257), ("P0", 1, 2), A.mult, ("P0", 0, 1), A.is_ge)
+        red(C("cnt"), R("AL", 0, 257))
+        ts(C("th"), C("cnt"), -256.0, A.add, ("P7", 1, 2), A.mult)
+        ts(C("th2"), C("th"), ("P7", 0, 1), A.add, C("h0"), A.add)
+        ts(R("GM"), R("JLC"), ("P0", 1, 2), A.mult, C("th2"), A.is_ge)
+        sc = 2.0 ** -12
+        for i, c in enumerate((("DD", 2, 3), ("DD", 4, 5), ("HL", 2, 3), ("HL", 3, 4), ("DD", 3, 4), ("DD", 5, 6), ("HL", 6, 7), ("HL", 7, 8))):
+            lt = ("LT", 128 * i, 128 * i + 128)
+            if c[0] == "DD":
+                ts(lt, R("GM"), c, A.mult, sc, A.mult)
+            else:
+                ts(lt, R("GM"), c, A.mult)
+            if i % 4 == 3:
+                pb, al = ("P1" if i == 3 else "P2"), ("AL", 0, 256)
+                mm([(pb, 256 * (x // 2), 256 * (x // 2) + 256, ("LT", 128 * (i - 3 + x), 128 * (i - 2 + x)), al, x % 2 == 0, x % 2 == 1) for x in range(4)])
+        for pb, r, x, o in (("P1", "RA", "XT", "XO"), ("P2", "RB", "YT", "YO")):
+            tt(R(x), (pb, 0, 256), R(r, 256 * t, 256 * t + 256), A.mult)
+            tt(R(x), (pb, 256, 512), R(x), A.add)
+            ts(R(o), R(x), M23 + 1920.0, A.add, M23, A.subtract)
+
+    def gath(o, c0, c1):
+        return (("BANK", 0, TR), (o, c0 // 16, c1 // 16))
+
+    def sumkey(w, bank, b0, q):
+        mm([(bank, b0, b0 + 64, (w, 128 * l, 128 * l + 128), ("CAND", 1024 * q + l, 1024 * q + 1024, 16), l == 0, l == 15) for l in range(16)])
+
+    def masks(c0, c1, pk):
+        cp(R("KI", c0, c1), (pk, 0, c1 - c0))
+        ts(R("OW", c0, c1), R("KI", c0, c1), 3, A.bitwise_and)
+        ts(R("DE", c0, c1), R("AB1", c0, c1), C("ld"), A.is_gt, 4.0, A.mult)
+        tt(R("DE", c0, c1), R("DE", c0, c1), R("OW", c0, c1), A.add)
+        for p in range(N):
+            ts(("FM", 256 * p + c0, 256 * p + c1), R("DE", c0, c1), float(p), A.is_equal)
+        for p in range(N):
+            f = ("FM", 256 * p + c0, 256 * p + c1)
+            scan(("SC",) + f[1:], f, f, ("SC", 256 * p + c0 - 1, 256 * p + c0) if c0 else 0.0, A.add, A.max)
+
+    def constants_a():
+        cp(R("UG"), R("KRI"))
+        dma("Y", T.UD[:, :], T.UG[:, 0:256], [R("UG")], [("UD", 0, 4096)])
+        for l in range(16):
+            dma("Y", T.USED[l::16, 0:Q], T.UD[:, :], [("UD", 0, 4096)], [("USED", 0, Q)] if l == 15 else [], "d11")
+        fill(R("LS"), 0.0)
+        for l in range(16):
+            cp(("LS", 128 * l + l, 128 * l + 128, 16), ("BO", 0, 128, 16))
+        ts(C("s4"), ("ip", 5, 6), -2.0, A.mult, 1.0, A.add)
+        ts(R("EL"), R("rowl"), C("l"), A.is_equal)
+        tt(R("IDN"), R("EL"), R("BO"), A.mult)
+        ts(R("NID"), R("IDN"), -1.0, A.mult)
+        ts(C("lb"), ("lims", 0, 1), ("lims", 1, 2), A.add, -1.0, A.mult)
+        ts(C("ld"), ("lims", 1, 2), ("lims", 0, 1), A.subtract)
+        ts(R("EL"), R("rowl"), C("l"), A.is_lt)
+        tt(R("UP"), R("EL"), R("BO"), A.mult)
+        ts(R("NU"), R("UP"), -1.0, A.mult)
+        ts(R("BO16"), R("BO"), 16.0, A.mult)
+        ts(R("BO256"), R("BO"), 256.0, A.mult)
+        ts(R("KP"), R("R256"), C("l"), A.is_equal, 32768.0, A.mult)
+        fill(R("CAND", J, J + DUM), -512.0)
+        fill(R("W2S", 64, 72), 1000000.0)
+        fill(R("W3S", 1024, 1040), 1000000.0)
+        ts(C("wi"), C("l"), 14.0, A.mult, 9.0, A.add)
+
+    def constants_b():
+        ts(R("EL"), R("rowl"), C("l"), A.is_gt)
+        tt(R("SU"), R("EL"), R("BO"), A.mult)
+        ts(R("WB"), R("BO"), C("wi"), A.mult)
+        ts(R("NBO"), R("BO"), -1.0, A.mult)
+        ts(R("MK2"), R("R256"), C("l"), A.not_equal, 9984.0, A.mult)
+        ts(R("RST"), R("R256"), 0.0, A.is_gt)
+        ts(R("I16"), R("I16"), C("l"), A.add)
+        ts(R("TB"), R("I16"), float(TR), A.add)
+        fill(R("ONE256"), 1.0)
+        fill(R("USED", TR, TR + 256), 1.0)
+
+    for t in range(RO):
+        land, send = "LAND%d" % t, "SEND%d" % t
+        if t:
+            lists_z(t)
+        act(R("TZ", 0, 1024), gath("ZO", 0, 1024), F.Copy)
+        act(R("TZ", 3072, 4096), gath("ZO", 3072, 4096), F.Copy)
+        if t == 0:
+            prepare(0)
+        decode_xy(t)
+        if t == 0:
+            constants_a()
+            act(R("WK4"), R("LS"), F.Copy, scale=C("s4"))
+        act(R("TX", 1024, 2048), gath("XO", 1024, 2048), F.Copy)
+        tt(R("TX", 0, 1024), gath("XO", 0, 1024), R("TZ", 0, 1024), A.min)
+        tt(R("CAND", 0, 1024), gath("YO", 0, 1024), R("TX", 0, 1024), A.min)
+        sumkey("LS", "P1", 0, 0)
+        sumkey("WK4", "P2", 0, 0)
+        act(R("TX", 2048, 3072), gath("XO", 2048, 3072), F.Copy)
+        act(R("TY", 2048, 3072), gath("YO", 2048, 3072), F.Copy)
+        for i in range(2):
+            c, pb = 2048 + 512 * i, "P%d" % (5 + i)
+            mm([(pb, 0, 512, R("IDN"), ("TX", c, c + 512), True, False), (pb, 0, 512, R("NID"), ("TY", c, c + 512), False, True)])
+        for i in range(2):
+            act(R("TZ", 2048 + 512 * i, 2560 + 512 * i), ("P%d" % (5 + i), 0, 512), F.Abs)
+        tt(R("TY", 1024, 2048), gath("YO", 1024, 2048), R("TX", 1024, 2048), A.max)
+        tt(R("CAND", 1024, 2048), gath("ZO", 1024, 2048), R("TY", 1024, 2048), A.min)
+        sumkey("LS", "P1", 64, 1)
+        sumkey("WK4", "P2", 64, 1)
+        for i in range(2):
+            c = 3072 + 512 * i
+            act(R("TX", c, c + 512), gath("XO", c, c + 512), F.Copy)
+            act(R("TY", c, c + 512), gath("YO", c, c + 512), F.Copy)
+        tt(R("CAND", 2048, 3072), gath("ZO", 2048, 3072), R("TZ", 2048, 3072), A.min)
+        for i in range(2):
+            c, pb = 3072 + 512 * i, ("P7", "P5")[i]
+            mm([(pb, 0, 512, R("IDN"), ("TX", c, c + 512), True, False), (pb, 0, 512, R("IDN"), ("TY", c, c + 512), False, True)])
+            sumkey(("LS", "WK4")[i], ("P1", "P2")[i], 128, 2)
+            tt(R("CAND", c, c + 512), (pb, 0, 512), R("TZ", c, c + 512), A.min)
+        sumkey("LS", "P3", 0, 3)
+        sumkey("WK4", "P4", 0, 3)
+        act(R("AB1", 0, 192), ("P1", 0, 192), F.Abs, scale=2.0, bias=C("lb"))
+        masks(0, 192, "P2")
+        act(R("AB1", 192, 256), ("P3", 0, 64), F.Abs, scale=2.0, bias=C("lb"))
+        masks(192, 256, "P4")
+        mm([("P0", 64, 128, R("BO"), ("SC", 15, 1024, 16), True, True)])
+        mm([("P7", 0, 64, ("LS", 128 * b, 128 * b + 128), ("SC", b, 1024, 16), b == 0, b == 15) for b in range(16)])
+        for i in range(2):
+            mm([("P%d" % (5 + i), 0, 512, R("BO"), ("SC", 512 * i, 512 * i + 512), True, False),
+                ("P%d" % (5 + i), 0, 512, R("NU"), ("FM", 512 * i, 512 * i + 512), False, True)])
+        act(R("W2S", 0, 64), ("P7", 0, 64), F.Copy)
+        for i in range(2):
+            act(R("W3S", 512 * i, 512 * i + 512), ("P%d" % (5 + i), 0, 512), F.Copy)
+        if t == 0:
+            act(R("WKF"), R("LS"), F.Copy, scale=C("wi"))
+        scan(R("W1T"), R("KP", 0, 64), ("P0", 64, 128), 0.0, A.max, A.min)
+        for p in range(N):
+            ts(("I1", 64 * p, 64 * p + 64), R("sB"), ("W1T", 16 * p + 15, 16 * p + 16), A.is_ge)
+        mm([("P1", 0, 256, R("BO"), R("I1"), True, True)])
+        mm([("P2", 0, 256, R("BO16"), R("I1"), True, False)])
+        mm([("P3", 0, 256, R("BO256"), R("I1"), True, False)])
+        scan(R("PK1"), R("KP"), ("P1", 0, 256), 0.0, A.max, A.min)
+        tt(R("O1"), ("PK1", 15, 256, 16), R("C16"), A.add)
+        tt(R("I2"), (("W2S", 0, 72), R("O1")), R("sR"), A.is_le)
+        mm([("P2", 0, 256, R("BO"), R("I2"), False, True)])
+        mm([("P3", 0, 256, R("BO16"), R("I2"), False, False)])
+        scan(R("PK2"), R("KP"), ("P2", 0, 256), 0.0, A.max, A.min)
+        tt(R("O2"), ("PK2", 15, 256, 16), R("C256"), A.add)
+        tt(R("I3"), (("W3S", 0, 1040), R("O2")), R("sR"), A.is_le)
+        mm([("P3", 0, 256, R("BO"), R("I3"), False, True)])
+        scan(R("PK3"), R("KP"), ("P3", 0, 256), 0.0, A.max, A.min)
+        cp(R("O3"), ("PK3", 15, 256, 16))
+        cp(R(send), (("CAND", 0, J + DUM), R("O3")))
+        deps("G", [R(send)], [])
+        tr, lo = [], 0
+        for d, ne in ((1, 4), (2, 4), (3, 8)):
+            p = (rank + d) % N
+            rid, pid = topo.addr(T.cores[p])[:2]
+            mask = sum(1 << x for x in topo.engines(core, T.cores[p])[lo:lo + ne])
+            lo += ne
+            tr.append(RemoteDMATransfer(dst_ids=[DstId(rid=rid, pnc=pid)], dma_engine_mask=mask, remote_sem=T.sem["arr%d" % t],
+                                        src=T[send][:, 64 * p:64 * p + 64], dst=T[land][:, 64 * rank:64 * rank + 64]))
+        g.remote_dma_fused(tr, local_sem=T.sem["snt%d" % t])
+        count["snt%d" % t] = 16
+        count["arr%d" % t] = 16
+        note("G", [], [(land, 64 * p, 64 * p + 64) for p in range(N) if p != rank], ("arr%d" % t, 16), True)
+        cp((land, 64 * rank, 64 * rank + 64), (send, 64 * rank, 64 * rank + 64))
+        if t == 0:
+            constants_b()
+        else:
+            cp((("USED", 0, TR + 256), R("UO2")), R("ONE256"))
+        tt(C("Tn"), C("Told"), C("e%d" % t), A.add)
+        cp(C("Told"), C("Tn"))
+        ts(R("TI"), R("I16"), C("Told"), A.add)
+        if t < RO - 1:
+            cp(("RN", 3 + t, 4 + t), C("e%d" % t))
+            prepare(t + 1)
+        mm([("P1", 0, 256, R("WB"), R(land), True, True)])
+        mm([("P2", 0, 16, ("WKF", 128 * l, 128 * l + 128), (land, l, 256, 16), l == 0, l == 15) for l in range(16)])
+        cp(R("KRI"), ("P1", 0, 256))
+        ts(R("BRI"), R("KRI"), 2, A.arith_shift_right, 4095, A.bitwise_and)
+        cp(R("BR"), R("BRI"))
+        cp(R("KBI"), ("P2", 0, 16))
+        ts(R("NV"), ("P2", 0, 16), 0.0, A.is_lt, 4096.0, A.mult)
+        ts(R("BBI"), R("KBI"), 2, A.arith_shift_right, 4095, A.bitwise_and)
+        tt(R("UO"), R("BBI"), R("NV"), A.add)
+        tt(R("BC"), R("BBI"), R("NV"), A.add)
+        act(R("UG"), (("USED", 0, TR + 256), R("UO")), F.Copy)
+        mm([("P3", 0, 256, R("BO"), R("UG"), True, False)])
+        for c in range(16):
+            o = 256 * c + 16 * c
+            ts(("E", o, 256 * c + 256), ("BR", 16 * c, 256), ("BC", c, c + 1), A.is_equal)
+            lst = [("P3", 16 * c, 16 * c + 16, R("SU"), ("E", o, o + 16), False, c == 15)]
+            if c < 15:
+                lst.append(("P3", 16 * c + 16, 256, R("BO"), ("E", o + 16, 256 * c + 256), False, False))
+            mm(lst)
+        tt(R("XP"), ("P3", 0, 256), R("MK2"), A.is_gt)
+        scan(R("XS"), R("RST"), R("XP"), 0.0, A.mult, A.add)
+        xs = ("XS", 15, 256, 16)
+        scan(R("SK"), xs, xs, 0.0, A.add, A.max)
+        mm([("P4", 0, 16, R("NBO"), R("SK"), True, False), ("P4", 0, 16, R("UP"), xs, False, True),
+            ("P4", 16, 17, R("NBO"), ("SK", 15, 16), True, True)])
+        tt(R("NK"), xs, R("TB"), A.mult)
+        tt(R("PO"), ("P4", 0, 16), R("TI"), A.add)
+        tt(R("SO"), R("PO"), R("NK"), A.max)
+        cp((("BANK", 0, TR + 256), R("SO")), R(land))
+        if t < RO - 1:
+            ts(C("e%d" % (t + 1)), ("P4", 16, 17), 256.0, A.add)
+            tt(R("UO2"), R("BC"), R("NK"), A.max)
+
+    dma("Y", T.y[:, :], T.BANK[:, B:TR], [("BANK", B, TR)], [])
+    for s in sorted(count):
+        g.wait_ge(T.sem[s], count[s])

@@ -17,13 +17,13 @@ def _sb(dtype, **kw):
         SCRATCH[n] = ("sbuf", [128, w], dtype)
 
 
-_sb("bfloat16", BANK=TR + 256, CAND=J + DUM, TX=J, TY=J, TZ=J, USED=TR + 256, ONE256=256, FM=1024, SC=1024, I1=256, I2=256, I3=256,
-    UG=256, E=4096, XP=256, XS=256, SK=16, SEND0=256, SEND1=256, SEND2=256, LAND0=256, LAND1=256, LAND2=256, BO=128, BO16=128,
-    BO256=128, NBO=128, IDN=128, NID=128, UP=128, NU=128, SU=128, WB=128, LS=2048, WK4=2048, WKF=2048, KP=256, MK2=256, RST=256,
-    rowg=128, rowl=128, rowk=128, rowh=128, R256=256, sB=64, IOC=258, JLC=128, AL=258, GM=128, LT=1024, EL=128)
-_sb("float32", sR=256, IC0=258, IC1=258, cols=64, RN=8, ra8=8, AS=8, M0=8, M1=8, AA=8, AB=8, T8=8, PRE=16, HL=16, DD=16, I16=16, TB=16,
-    TI=16, NK=16, C16=16, C256=16, W1T=64, W2S=72, W3S=1040, PK1=256, PK2=256, PK3=256, SEL8=128, NF=8, lims=8, TRI=128, TRIS=128,
-    ONE=128, ONES=128, rk6=128, F1=128, F2=128, ZT=256, XT=256, YT=256, AB1=256, DE=256, BC=16, NV=16, PO=16)
+_sb("bfloat16", BANK=TR + 256, CAND=J + DUM, TX=J, TY=J, TZ=J, USED=TR + 256, ONE256=256, FM=1024, SC=1024, I1=256, I2=256,
+    UG=256, E=4096, ED=256, XP=256, XS=256, SEND0=256, SEND1=256, SEND2=256, LAND0=256, LAND1=256, LAND2=256, BO=128, BO16=128,
+    BO256=128, NBO=128, IDN=128, NID=128, ID4=128, UP=128, NU=128, SU=128, WB=128, LS=2048, WKF=2048, WT=16, KP=256, MK2=256, RST=256,
+    rowg=128, rowl=128, rowk=128, rowh=128, R256=256, sB=64, IOC=258, JLC=128, AL=258, GM=128, LT=1024, X1=256, X2=256, OB=256)
+_sb("float32", sR=256, IC0=256, cols=64, RN=8, ra8=8, AS=8, M0=8, M1=8, AA=8, AB=8, T8=8, PRE=16, HL=16, DD=16, I16=16, TB=16,
+    TI=16, NK=16, C16=16, C256=16, W1T=64, W2S=72, W3S=1040, PK1=256, PK2=256, PK3=256, SEL8=128, NF=8, LX=256, LOT=128, HIT=128,
+    TRI=128, TRIS=128, ONE=128, ONES=128, rk6=128, F1=128, F1b=128, ZT=256, XT=256, YT=256, BC=16, NV=16, PO=16)
 _sb("int32", RA=768, RB=768, RC=768, ip=8, NI=8, WI=4, KI=256, OW=256, KRI=256, BRI=256, KBI=16, BBI=16)
 _sb("uint16", XO=256, YO=256, ZO=256, O1=16, O2=16, O3=16, UO=16, SO=16, UO2=16, BR=256)
 SCRATCH["UD"] = ("dram", [8, 4096], "bfloat16")
@@ -79,14 +79,16 @@ def rank_program(g, core, T, topo):
         note(q, reads, writes, (s, count[s]))
 
     def mm(lst):
-        reads = [x[3] for x in lst] + [x[4][:3] for x in lst]
+        reads = [x[3][:3] for x in lst] + [x[4][:3] for x in lst]
         writes = [x[:3] for x in lst]
         deps("P", reads, writes)
         last = None
-        for o, c0, c1, lh, rh, st, sp in lst:
+        for x in lst:
+            o, c0, c1, lh, rh, st, sp = x[:7]
             kp = rh[4] if len(rh) > 4 else 128
-            step = rh[3] if len(rh) > 3 else 1
-            last = g.tensor.matmul(T[o][:, c0:c1], T[lh[0]][0:kp, lh[1]:lh[2]], T[rh[0]][0:kp, rh[1]:rh[2]:step], st, sp)
+            lv = T[lh[0]][0:kp, lh[1]:lh[2]:lh[3] if len(lh) > 3 else 1]
+            rv = T[rh[0]][0:kp, rh[1]:rh[2]:rh[3] if len(rh) > 3 else 1]
+            last = g.tensor.matmul(T[o][:, c0:c1:x[7] if len(x) > 7 else 1], lv, rv, st, sp)
         count["cP"] = count.get("cP", 0) + 1
         last.then_inc(T.sem["cP"], 1)
         note("P", reads, writes, ("cP", count["cP"]))
@@ -142,14 +144,20 @@ def rank_program(g, core, T, topo):
     def fill(r, c):
         do("V", lambda: g.vector.memset(ap(r), c), [], regs(r))
 
-    def act(out, in0, func, scale=1.0, bias=0.0):
-        do("S", lambda: g.scalar.activation(ap(out), view(in0), func, bias=view(bias), scale=view(scale)), regs(in0, scale, bias), regs(out))
+    def act(out, in0, func=F.Copy, scale=1.0):
+        do("S", lambda: g.scalar.activation(ap(out), view(in0), func, bias=0.0, scale=view(scale)), regs(in0, scale), regs(out))
 
-    def iota(r, pattern, cm=0):
+    def lin(out, in0, scale, bias):
+        do("S", lambda: g.scalar.activation(ap(out), view(in0), F.Identity, bias=view(bias), scale=view(scale)), regs(in0, scale, bias), regs(out))
+
+    def iota(r, pattern, base=0, cm=0):
         if SCRATCH[r[0]][2] == "int32":
-            do("G", lambda: g.iota(ap(r), pattern, 0, cm), [], regs(r))
+            do("G", lambda: g.iota(ap(r), pattern, base, cm), [], regs(r))
         else:
-            do("G", lambda: g.iota(ap(r), pattern, 0, cm, allow_small_or_imprecise_dtypes=True), [], regs(r))
+            do("G", lambda: g.iota(ap(r), pattern, base, cm, allow_small_or_imprecise_dtypes=True), [], regs(r))
+
+    def sel(out, in0, pattern, op, fl, base, cm):
+        do("G", lambda: g.affine_select(ap(out), ap(in0), pattern, op, fl, base, cm), regs(in0), regs(out))
 
     def R(b, lo=0, hi=None, *step):
         return (b, lo, SCRATCH[b][1][1] if hi is None else hi) + step
@@ -174,68 +182,73 @@ def rank_program(g, core, T, topo):
     dma("Y", T.KRI[:, 0:256], T.used[:, :], [], [R("KRI")])
 
     ip = ("ip", 0, 1)
-    iota(ip, [[0, 1]], 1)
-    for b, pat in (("SEL8", [[1, 8], [0, 16]]), ("rowg", [[1, 8], [0, 16]]), ("ra8", [[1, 8]]), ("rowk", [[0, 16], [1, 8]]), ("rowl", [[0, 8], [1, 16]]),
-                   ("rowh", [[0, 8], [1, 2], [0, 8]])):
-        iota(R(b), pat)
-    iota(R("IC0", 0, 257), [[1, 257]])
-    for b, pat in (("R256", [[0, 16], [1, 16]]), ("sB", [[1, 64]]), ("sR", [[0, 4], [1, 64]]), ("I16", [[16, 16]]), ("C16", [[16, 4], [0, 4]]),
-                   ("C256", [[256, 4], [0, 4]])):
-        iota(R(b), pat)
-    fill(R("BANK", B, TR + 256), 0.0)
-    fill(R("RN"), 0.0)
+    iota(ip, [[0, 1]], 0, 1)
+    iota(R("rowg"), [[1, 8], [0, 16]])
+    iota(R("SEL8"), [[1, 8], [0, 16]])
+    iota(R("rowk"), [[0, 16], [1, 8]])
+    sel(R("rk6"), R("rowk"), [[0, 16], [-1, 8]], A.is_ge, -100.0, 5, 0)
+    iota(R("ra8"), [[1, 8]])
+    iota(R("rowl"), [[0, 8], [1, 16]])
+    iota(R("rowh"), [[0, 8], [2, 2], [0, 8]], -1)
+    iota(R("IC0"), [[1, 256]])
+    iota(R("BANK", B, TR + 256), [[0, 1024]])
+    iota(R("GM"), [[0, 128]], 1)
+    sel(R("IDN"), R("GM"), [[-1, 128]], A.is_equal, 0.0, 0, 1)
+    iota(R("R256"), [[0, 16], [1, 16]])
+    iota(R("CAND", J, J + DUM), [[0, DUM]], -512)
+    iota(R("W2S", 64, 72), [[0, 8]], 1000000)
+    iota(R("W3S", 1024, 1040), [[0, 16]], 1000000)
+    iota(R("LS"), [[0, 2048]])
+    iota(R("sB"), [[1, 64]])
+    iota(R("sR"), [[0, 4], [1, 64]])
+    iota(R("C16"), [[16, 4], [0, 4]])
+    iota(R("C256"), [[256, 4], [0, 4]])
+    iota(R("I16"), [[16, 16]])
+    iota(R("ONE256"), [[0, 256]], 1)
+    iota(R("USED", TR, TR + 256), [[0, 256]], 1)
+
     ts(("ip", 1, 2), ip, 15, A.bitwise_and)
     ts(("ip", 2, 3), ip, 7, A.bitwise_and)
     ts(("ip", 3, 4), ip, 3, A.logical_shift_right, 1, A.bitwise_and)
     ts(("ip", 4, 5), ip, 4, A.logical_shift_right)
     ts(("ip", 5, 6), ip, 1, A.bitwise_and)
-    for i, c in enumerate("plkhg"):
-        cp(C(c), ("ip", i, i + 1))
-    ts(R("SEL8"), R("SEL8"), C("p"), A.is_equal)
+    for c in "plkhgq":
+        C(c)
+    cp(("cols", 0, 6), ("ip", 0, 6))
     ts(R("BO"), R("rowg"), C("g"), A.is_equal)
-    ts(C("km1"), C("k"), -1.0, A.add)
-    ts(C("k6"), C("k"), 6.0, A.is_ge, 100.0, A.mult)
-    tt(C("kk"), C("k"), C("k6"), A.add)
-    ts(C("m0"), C("k"), 0.0, A.is_equal)
-    ts(C("m1"), C("k"), 1.0, A.is_equal)
-    tt(C("m01"), C("m0"), C("m1"), A.subtract)
-    ts(C("h0"), C("h"), -1.0, A.mult, 1.0, A.add)
-    ts(C("h0a"), C("h0"), 4096.0, A.mult)
-    ts(C("h0b"), C("h0"), 16.0, A.mult)
-    ts(C("sg16"), C("h"), 0.125, A.mult, -0.0625, A.add)
-    ts(C("k7h"), C("k"), 7.0, A.is_equal, C("h0"), A.mult)
-    ts(C("k6h"), C("k"), 6.0, A.is_equal, C("h0"), A.mult)
-    ts(C("chi"), C("k7h"), -1920.0, A.mult)
-    ts(C("clo"), C("k6h"), EPS, A.mult)
-    ts(C("k7m"), C("k7h"), -0.5, A.mult)
-    tt(C("clo"), C("clo"), C("k7m"), A.add)
-    for t in range(RO):
-        ts(C("ml%d" % t), C("k"), float(3 + t), A.is_equal)
-    ts(R("M0"), R("ra8"), C("k"), A.is_equal)
-    ts(R("M1"), R("ra8"), C("km1"), A.is_equal)
-    ts(R("AS"), R("ra8"), C("kk"), A.add)
-    ts(R("rk6"), R("rowk"), 6.0, A.is_ge, -100.0, A.mult)
-    tt(R("rk6"), R("rk6"), R("rowk"), A.add)
-    ts(R("F1"), R("rk6"), C("k"), A.is_gt, C("h0a"), A.mult)
-    tt(R("TRI"), R("F1"), R("BO"), A.mult)
-    ts(R("ONE"), R("BO"), C("h0b"), A.mult)
-    ts(R("F2"), R("rowh"), 2.0, A.mult, -1.0, A.add)
-    tt(R("TRIS"), R("TRI"), R("F2"), A.mult)
-    tt(R("ONES"), R("ONE"), R("F2"), A.mult)
-    ts(R("IC0", 0, 257), R("IC0", 0, 257), C("h"), A.add)
-    ts(R("IC1", 0, 257), R("IC0", 0, 257), 257.0, A.is_equal, -257.0, A.mult)
-    tt(R("IOC", 0, 257), R("IC0", 0, 257), R("IC1", 0, 257), A.add)
-    ts(R("F1"), R("rowl"), C("sg16"), A.mult)
-    tt(R("F1"), R("F1"), R("BO"), A.mult)
-    ts(R("F2"), R("BO"), 1024.0, A.mult, -1024.0, A.add)
-    tt(R("JLC"), R("F1"), R("F2"), A.add)
+    ts(R("SEL8"), R("SEL8"), C("p"), A.is_equal)
     do("V", lambda: g.vector.tensor_copy(T.NF[0:8, 0:6], T.NI[0:8, 0:6]), [("NI", 0, 6)], [("NF", 0, 6)])
     mm([("P0", 8, 14, ("SEL8", 0, 128), ("NF", 0, 6, 1, 8), True, True)])
+    lin(C("h0"), C("h"), -1.0, 1.0)
+    act(R("BO256"), R("BO"), scale=256.0)
+    lin(C("sg16"), C("h"), 0.125, -0.0625)
+    ts(R("F1"), R("rk6"), C("k"), A.is_gt, C("h0"), A.mult)
+    tt(R("TRI"), R("F1"), R("BO256"), A.mult)
+    act(R("ONE"), R("BO"), scale=C("h0"))
+    lin(R("F1b"), R("rowl"), C("sg16"), 1024.0)
+    lin(R("IOC", 0, 256), R("IC0"), 1.0, C("h"))
+    lin(R("IOC", 256, 257), C("h"), -256.0, 256.0)
+    ts(R("M0"), R("ra8"), C("k"), A.is_equal)
+    ts(R("M1"), R("ra8"), C("k"), A.subtract, -1.0, A.is_equal)
+    ts(C("k6"), C("k"), 6.0, A.is_ge, 100.0, A.mult)
+    tt(C("kk"), C("k"), C("k6"), A.add)
+    ts(R("AS"), R("ra8"), C("kk"), A.add)
+    m0 = ("M0", 0, 1)
+    tt(C("m01"), m0, ("M0", 1, 2), A.subtract)
+    act(C("c7"), ("M0", 7, 8), scale=C("h0"))
+    act(C("c6"), ("M0", 6, 7), scale=C("h0"))
+    act(C("chi"), C("c7"), scale=-1920.0)
+    act(C("c6"), C("c6"), scale=EPS)
+    lin(C("clo"), C("c7"), -0.5, C("c6"))
+    fill(R("RN"), 0.0)
+    act(("RN", 0, 3), ("P0", 8, 11))
+    act(C("e0"), ("P0", 11, 12))
+    lin(C("Told"), C("e0"), -1.0, float(B))
     lists_z(0)
-    cp(("RN", 0, 3), ("P0", 8, 11))
-    cp(C("e0"), ("P0", 11, 12))
-    cp(("lims", 0, 2), ("P0", 12, 14))
-    ts(C("Told"), C("e0"), -1.0, A.mult, float(B), A.add)
+    tt(R("TRIS"), R("TRI"), R("rowh"), A.mult)
+    tt(R("ONES"), R("ONE"), R("rowh"), A.mult)
+    tt(R("F1"), R("F1b"), R("BO"), A.mult)
+    lin(R("JLC"), R("F1"), 1.0, -1024.0)
 
     def prepare(t):
         s = 4 + t
@@ -246,36 +259,42 @@ def rank_program(g, core, T, topo):
             red(C(c), R("T8"))
         tt(("PRE", 0, 1), C("PNL"), C("dS"), A.subtract)
         tt(("PRE", 1, 2), C("PNR"), C("Qc"), A.subtract)
-        ts(C("dSb"), C("m0"), C("Told"), A.mult, C("PNR"), A.subtract)
+        ts(C("dSb"), m0, C("Told"), A.mult, C("PNR"), A.subtract)
         for c, i in (("dS", 2), ("dSb", 6)):
-            ts(("HL", i, i + 1), C(c), M27, A.add, M27, A.subtract)
-            tt(("HL", i + 1, i + 2), C(c), ("HL", i, i + 1), A.subtract)
-            tt(("HL", i, i + 1), ("HL", i, i + 1), C("chi"), A.add)
-            tt(("HL", i + 1, i + 2), ("HL", i + 1, i + 2), C("clo"), A.add)
+            hi, lo = ("HL", i, i + 1), ("HL", i + 1, i + 2)
+            lin(lo, C(c), 1.0, M27)
+            lin(hi, lo, 1.0, -M27)
+            lin(lo, hi, -1.0, C(c))
+            lin(lo, lo, 1.0, C("clo"))
+            lin(hi, hi, 1.0, C("chi"))
+
+    def newest(t):
+        e = C("e%d" % t)
+        for i, m in enumerate((("M0", 3 + t, 4 + t), C("m01"))):
+            lin(("DD", i, i + 1), m, e, ("PRE", i, i + 1))
+        lin(("DD", 6, 8), ("DD", 0, 2), 1.0, M27)
+        lin(("DD", 2, 4), ("DD", 6, 8), 1.0, -M27)
+        for i in range(2):
+            lin(("DD", 4 + i, 5 + i), ("DD", 2 + i, 3 + i), -1.0, ("DD", i, i + 1))
 
     def decode_xy(t):
-        e = C("e%d" % t)
-        ts(C("NL"), C("ml%d" % t), e, A.mult, C("PNL"), A.add)
-        ts(C("NR"), C("m0"), e, A.mult, C("PNR"), A.add)
+        e, ml = C("e%d" % t), ("M0", 3 + t, 4 + t)
+        ts(C("NL"), ml, e, A.mult, C("PNL"), A.add)
+        ts(C("NR"), m0, e, A.mult, C("PNR"), A.add)
         tt(("WI", 0, 1), C("NL"), C("NR"), A.mult)
         ts(("WI", 1, 2), ("WI", 0, 1), 12, A.arith_shift_right)
-        cp(C("w"), ("WI", 1, 2))
+        ts(C("w"), ("WI", 1, 2), 16.0, A.mult)
         mm([("P0", 0, 1, R("TRI"), C("w"), True, True), ("P0", 1, 2, R("ONE"), C("w"), True, True)])
         mm([("P7", 0, 1, R("TRIS"), C("w"), True, True), ("P7", 1, 2, R("ONES"), C("w"), True, True)])
-        ts(("DD", 0, 1), C("ml%d" % t), e, A.mult, ("PRE", 0, 1), A.add)
-        ts(("DD", 1, 2), C("m01"), e, A.mult, ("PRE", 1, 2), A.add)
-        ts(("DD", 2, 4), ("DD", 0, 2), M27, A.add, M27, A.subtract)
-        tt(("DD", 4, 6), ("DD", 0, 2), ("DD", 2, 4), A.subtract)
         ts(R("AL", 0, 257), R("IOC", 0, 257), ("P0", 1, 2), A.mult, ("P0", 0, 1), A.is_ge)
         red(C("cnt"), R("AL", 0, 257))
         ts(C("th"), C("cnt"), -256.0, A.add, ("P7", 1, 2), A.mult)
         ts(C("th2"), C("th"), ("P7", 0, 1), A.add, C("h0"), A.add)
         ts(R("GM"), R("JLC"), ("P0", 1, 2), A.mult, C("th2"), A.is_ge)
-        sc = 2.0 ** -12
         for i, c in enumerate((("DD", 2, 3), ("DD", 4, 5), ("HL", 2, 3), ("HL", 3, 4), ("DD", 3, 4), ("DD", 5, 6), ("HL", 6, 7), ("HL", 7, 8))):
             lt = ("LT", 128 * i, 128 * i + 128)
             if c[0] == "DD":
-                ts(lt, R("GM"), c, A.mult, sc, A.mult)
+                ts(lt, R("GM"), c, A.mult, 2.0 ** -12, A.mult)
             else:
                 ts(lt, R("GM"), c, A.mult)
             if i % 4 == 3:
@@ -289,126 +308,138 @@ def rank_program(g, core, T, topo):
     def gath(o, c0, c1):
         return (("BANK", 0, TR), (o, c0 // 16, c1 // 16))
 
-    def sumkey(w, bank, b0, q):
-        mm([(bank, b0, b0 + 64, (w, 128 * l, 128 * l + 128), ("CAND", 1024 * q + l, 1024 * q + 1024, 16), l == 0, l == 15) for l in range(16)])
+    def sg(b, o, c, n):
+        act(R(b, c, c + n), gath(o, c, c + n))
 
-    def masks(c0, c1, pk):
-        cp(R("KI", c0, c1), (pk, 0, c1 - c0))
-        ts(R("OW", c0, c1), R("KI", c0, c1), 3, A.bitwise_and)
-        ts(R("DE", c0, c1), R("AB1", c0, c1), C("ld"), A.is_gt, 4.0, A.mult)
-        tt(R("DE", c0, c1), R("DE", c0, c1), R("OW", c0, c1), A.add)
+    def add2(pb, c, n, w):
+        mm([(pb, 0, n, R("IDN"), ("TX", c, c + n), True, False), (pb, 0, n, R(w), ("TY", c, c + n), False, True)])
+
+    def sumkey(h):
+        mm([("P%d" % (1 + h), l, 256, ("CAND", 2048 * h + l, 2048 * h + 2048, 16), R("WT"), True, True, 16) for l in range(16)])
+
+    def codes(h):
+        pb, a = "P%d" % (1 + h), (128 * h, 128 * h + 128)
+        cp(R("KI", *a), (pb, 128, 256))
+        tt(R("X1", *a), (pb, 0, 128), R("LOT"), A.is_lt)
+        tt(R("X2", *a), (pb, 0, 128), R("HIT"), A.is_gt)
+        ts(R("OW", *a), R("KI", *a), 3, A.bitwise_and)
+        cp(R("OB", *a), R("OW", *a))
+        pc = "P%d" % (3 + h)
+        mm([(pc, 0, 128, R("X1", *a), R("ID4"), True, False), (pc, 0, 128, R("X2", *a), R("ID4"), False, False),
+            (pc, 0, 128, R("OB", *a), R("IDN"), False, True)])
+
+    def part(h):
+        return [(256 * p + 128 * h, 256 * p + 128 * h + 128) for p in range(N)]
+
+    def masks(h):
+        for p, f in enumerate(part(h)):
+            ts(("FM",) + f, ("P%d" % (3 + h), 0, 128), float(p), A.is_equal)
+
+    def scans(h):
+        for f in part(h):
+            scan(("SC",) + f, ("FM",) + f, ("FM",) + f, ("SC", f[0] - 1, f[0]) if h else 0.0, A.add, A.max)
+
+    def counts(h):
         for p in range(N):
-            ts(("FM", 256 * p + c0, 256 * p + c1), R("DE", c0, c1), float(p), A.is_equal)
+            pb, o, c = "P%d" % (5 + p // 2), 256 * (p % 2) + 128 * h, 256 * p + 128 * h
+            mm([(pb, o, o + 128, R("BO"), ("SC", c, c + 128), True, False), (pb, o, o + 128, R("NU"), ("FM", c, c + 128), False, True)])
         for p in range(N):
-            f = ("FM", 256 * p + c0, 256 * p + c1)
-            scan(("SC",) + f[1:], f, f, ("SC", 256 * p + c0 - 1, 256 * p + c0) if c0 else 0.0, A.add, A.max)
-
-    def constants_a():
-        cp(R("UG"), R("KRI"))
-        dma("Y", T.UD[:, :], T.UG[:, 0:256], [R("UG")], [("UD", 0, 4096)])
-        for l in range(16):
-            dma("Y", T.USED[l::16, 0:Q], T.UD[:, :], [("UD", 0, 4096)], [("USED", 0, Q)] if l == 15 else [], "d11")
-        fill(R("LS"), 0.0)
-        for l in range(16):
-            cp(("LS", 128 * l + l, 128 * l + 128, 16), ("BO", 0, 128, 16))
-        ts(C("s4"), ("ip", 5, 6), -2.0, A.mult, 1.0, A.add)
-        ts(R("EL"), R("rowl"), C("l"), A.is_equal)
-        tt(R("IDN"), R("EL"), R("BO"), A.mult)
-        ts(R("NID"), R("IDN"), -1.0, A.mult)
-        ts(C("lb"), ("lims", 0, 1), ("lims", 1, 2), A.add, -1.0, A.mult)
-        ts(C("ld"), ("lims", 1, 2), ("lims", 0, 1), A.subtract)
-        ts(R("EL"), R("rowl"), C("l"), A.is_lt)
-        tt(R("UP"), R("EL"), R("BO"), A.mult)
-        ts(R("NU"), R("UP"), -1.0, A.mult)
-        ts(R("BO16"), R("BO"), 16.0, A.mult)
-        ts(R("BO256"), R("BO"), 256.0, A.mult)
-        ts(R("KP"), R("R256"), C("l"), A.is_equal, 32768.0, A.mult)
-        fill(R("CAND", J, J + DUM), -512.0)
-        fill(R("W2S", 64, 72), 1000000.0)
-        fill(R("W3S", 1024, 1040), 1000000.0)
-        ts(C("wi"), C("l"), 14.0, A.mult, 9.0, A.add)
-
-    def constants_b():
-        ts(R("EL"), R("rowl"), C("l"), A.is_gt)
-        tt(R("SU"), R("EL"), R("BO"), A.mult)
-        ts(R("WB"), R("BO"), C("wi"), A.mult)
-        ts(R("NBO"), R("BO"), -1.0, A.mult)
-        ts(R("MK2"), R("R256"), C("l"), A.not_equal, 9984.0, A.mult)
-        ts(R("RST"), R("R256"), 0.0, A.is_gt)
-        ts(R("I16"), R("I16"), C("l"), A.add)
-        ts(R("TB"), R("I16"), float(TR), A.add)
-        fill(R("ONE256"), 1.0)
-        fill(R("USED", TR, TR + 256), 1.0)
+            pb, o, c = "P%d" % (5 + p // 2), 256 * (p % 2) + 128 * h, 256 * p + 128 * h
+            act(R("W3S", c, c + 128), (pb, o, o + 128))
 
     for t in range(RO):
         land, send = "LAND%d" % t, "SEND%d" % t
         if t:
             lists_z(t)
-        act(R("TZ", 0, 1024), gath("ZO", 0, 1024), F.Copy)
-        act(R("TZ", 3072, 4096), gath("ZO", 3072, 4096), F.Copy)
+            newest(t)
+        sg("TZ", "ZO", 0, 1024)
         if t == 0:
             prepare(0)
+            newest(0)
+        sg("TZ", "ZO", 3072, 1024)
         decode_xy(t)
         if t == 0:
-            constants_a()
-            act(R("WK4"), R("LS"), F.Copy, scale=C("s4"))
-        act(R("TX", 1024, 2048), gath("XO", 1024, 2048), F.Copy)
+            cp(R("UG"), R("KRI"))
+            dma("Y", T.UD[:, :], T.UG[:, 0:256], [R("UG")], [("UD", 0, 4096)])
+            for l in range(16):
+                dma("Y", T.USED[l::16, 0:Q], T.UD[:, :], [("UD", 0, 4096)], [("USED", 0, Q)] if l == 15 else [], "d11")
+            act(R("NID"), R("IDN"), scale=-1.0)
+        sg("TX", "XO", 1024, 1024)
         tt(R("TX", 0, 1024), gath("XO", 0, 1024), R("TZ", 0, 1024), A.min)
         tt(R("CAND", 0, 1024), gath("YO", 0, 1024), R("TX", 0, 1024), A.min)
-        sumkey("LS", "P1", 0, 0)
-        sumkey("WK4", "P2", 0, 0)
-        act(R("TX", 2048, 3072), gath("XO", 2048, 3072), F.Copy)
-        act(R("TY", 2048, 3072), gath("YO", 2048, 3072), F.Copy)
         for i in range(2):
-            c, pb = 2048 + 512 * i, "P%d" % (5 + i)
-            mm([(pb, 0, 512, R("IDN"), ("TX", c, c + 512), True, False), (pb, 0, 512, R("NID"), ("TY", c, c + 512), False, True)])
+            c = 2048 + 512 * i
+            sg("TX", "XO", c, 512)
+            sg("TY", "YO", c, 512)
+            add2("P%d" % (5 + i), c, 512, "NID")
+        sg("TX", "XO", 3072, 512)
         for i in range(2):
             act(R("TZ", 2048 + 512 * i, 2560 + 512 * i), ("P%d" % (5 + i), 0, 512), F.Abs)
         tt(R("TY", 1024, 2048), gath("YO", 1024, 2048), R("TX", 1024, 2048), A.max)
         tt(R("CAND", 1024, 2048), gath("ZO", 1024, 2048), R("TY", 1024, 2048), A.min)
-        sumkey("LS", "P1", 64, 1)
-        sumkey("WK4", "P2", 64, 1)
-        for i in range(2):
-            c = 3072 + 512 * i
-            act(R("TX", c, c + 512), gath("XO", c, c + 512), F.Copy)
-            act(R("TY", c, c + 512), gath("YO", c, c + 512), F.Copy)
-        tt(R("CAND", 2048, 3072), gath("ZO", 2048, 3072), R("TZ", 2048, 3072), A.min)
-        for i in range(2):
-            c, pb = 3072 + 512 * i, ("P7", "P5")[i]
-            mm([(pb, 0, 512, R("IDN"), ("TX", c, c + 512), True, False), (pb, 0, 512, R("IDN"), ("TY", c, c + 512), False, True)])
-            sumkey(("LS", "WK4")[i], ("P1", "P2")[i], 128, 2)
-            tt(R("CAND", c, c + 512), (pb, 0, 512), R("TZ", c, c + 512), A.min)
-        sumkey("LS", "P3", 0, 3)
-        sumkey("WK4", "P4", 0, 3)
-        act(R("AB1", 0, 192), ("P1", 0, 192), F.Abs, scale=2.0, bias=C("lb"))
-        masks(0, 192, "P2")
-        act(R("AB1", 192, 256), ("P3", 0, 64), F.Abs, scale=2.0, bias=C("lb"))
-        masks(192, 256, "P4")
-        mm([("P0", 64, 128, R("BO"), ("SC", 15, 1024, 16), True, True)])
-        mm([("P7", 0, 64, ("LS", 128 * b, 128 * b + 128), ("SC", b, 1024, 16), b == 0, b == 15) for b in range(16)])
-        for i in range(2):
-            mm([("P%d" % (5 + i), 0, 512, R("BO"), ("SC", 512 * i, 512 * i + 512), True, False),
-                ("P%d" % (5 + i), 0, 512, R("NU"), ("FM", 512 * i, 512 * i + 512), False, True)])
-        act(R("W2S", 0, 64), ("P7", 0, 64), F.Copy)
-        for i in range(2):
-            act(R("W3S", 512 * i, 512 * i + 512), ("P%d" % (5 + i), 0, 512), F.Copy)
         if t == 0:
-            act(R("WKF"), R("LS"), F.Copy, scale=C("wi"))
+            cp(R("WT", 0, 8), ("BO", 0, 128, 16))
+            ts(C("s4"), C("q"), -2.0, A.mult, 1.0, A.add)
+            ts(R("WT", 8, 16), R("WT", 0, 8), C("s4"), A.mult)
+        sumkey(0)
+        tt(R("CAND", 2048, 3072), gath("ZO", 2048, 3072), R("TZ", 2048, 3072), A.min)
+        sg("TY", "YO", 3072, 512)
+        for c in (3584, 3840):
+            sg("TX", "XO", c, 256)
+            sg("TY", "YO", c, 256)
+        if t == 0:
+            act(R("ID4"), R("IDN"), scale=4.0)
+            for i, b in ((4, "LOT"), (5, "HIT")):
+                li, o = ("LX", 128 * (i - 4), 128 * (i - 4) + 128), 128 * (i - 3)
+                do("V", lambda: g.vector.tensor_scalar(T.LX[0:8, li[1]:li[2]], T.SEL8[0:8, 0:128], 0.0, T.NF[0:8, i:i + 1], A.mult, A.add),
+                   [R("SEL8"), ("NF", i, i + 1)], [li])
+                mm([("P0", o, o + 128, li, ("SEL8", 0, 128, 1, 8), True, True)])
+                act(R(b), ("P0", o, o + 128))
+        for c, n, pb in ((3072, 512, "P7"), (3584, 256, "P5"), (3840, 256, "P6")):
+            add2(pb, c, n, "IDN")
+            if c == 3072:
+                codes(0)
+            tt(R("CAND", c, c + n), (pb, 0, n), R("TZ", c, c + n), A.min)
+        sumkey(1)
+        if t == 0:
+            sel(R("UP"), R("BO"), [[-1, 128]], A.is_gt, 0.0, 0, 1)
+            sel(R("SU"), R("BO"), [[1, 128]], A.is_gt, 0.0, 0, -1)
+            act(R("NU"), R("UP"), scale=-1.0)
+            act(R("BO16"), R("BO"), scale=16.0)
+            for l in range(16):
+                act(("LS", 128 * l + l, 128 * l + 128, 16), ("BO", 0, 128, 16))
+            ts(R("KP"), R("R256"), C("l"), A.is_equal, 32768.0, A.mult)
+        masks(0)
+        codes(1)
+        scans(0)
+        counts(0)
+        masks(1)
+        scans(1)
+        mm([("P0", 64, 128, R("BO"), ("SC", 15, 1024, 16), True, True)])
+        mm([("P7", 0, 64, ("LS", 128 * b, 128 * b + 128), ("SC", b, 1024, 16), b == 0, False) for b in range(11)])
         scan(R("W1T"), R("KP", 0, 64), ("P0", 64, 128), 0.0, A.max, A.min)
         for p in range(N):
             ts(("I1", 64 * p, 64 * p + 64), R("sB"), ("W1T", 16 * p + 15, 16 * p + 16), A.is_ge)
         mm([("P1", 0, 256, R("BO"), R("I1"), True, True)])
+        mm([("P7", 0, 64, ("LS", 128 * b, 128 * b + 128), ("SC", b, 1024, 16), False, b == 15) for b in range(11, 16)])
+        act(R("W2S", 0, 64), ("P7", 0, 64))
         mm([("P2", 0, 256, R("BO16"), R("I1"), True, False)])
-        mm([("P3", 0, 256, R("BO256"), R("I1"), True, False)])
+        counts(1)
         scan(R("PK1"), R("KP"), ("P1", 0, 256), 0.0, A.max, A.min)
         tt(R("O1"), ("PK1", 15, 256, 16), R("C16"), A.add)
         tt(R("I2"), (("W2S", 0, 72), R("O1")), R("sR"), A.is_le)
         mm([("P2", 0, 256, R("BO"), R("I2"), False, True)])
+        mm([("P3", 0, 256, R("BO256"), R("I1"), True, False)])
         mm([("P3", 0, 256, R("BO16"), R("I2"), False, False)])
+        if t == 0:
+            ts(C("wi"), C("l"), 14.0, A.mult, 9.0, A.add)
+            act(R("WB"), R("BO"), scale=C("wi"))
+            act(R("WKF"), R("LS"), scale=C("wi"))
+            act(R("NBO"), R("BO"), scale=-1.0)
         scan(R("PK2"), R("KP"), ("P2", 0, 256), 0.0, A.max, A.min)
         tt(R("O2"), ("PK2", 15, 256, 16), R("C256"), A.add)
-        tt(R("I3"), (("W3S", 0, 1040), R("O2")), R("sR"), A.is_le)
-        mm([("P3", 0, 256, R("BO"), R("I3"), False, True)])
+        tt(R("XP"), (("W3S", 0, 1040), R("O2")), R("sR"), A.is_le)
+        mm([("P3", 0, 256, R("BO"), R("XP"), False, True)])
         scan(R("PK3"), R("KP"), ("P3", 0, 256), 0.0, A.max, A.min)
         cp(R("O3"), ("PK3", 15, 256, 16))
         cp(R(send), (("CAND", 0, J + DUM), R("O3")))
@@ -427,7 +458,10 @@ def rank_program(g, core, T, topo):
         note("G", [], [(land, 64 * p, 64 * p + 64) for p in range(N) if p != rank], ("arr%d" % t, 16), True)
         cp((land, 64 * rank, 64 * rank + 64), (send, 64 * rank, 64 * rank + 64))
         if t == 0:
-            constants_b()
+            ts(R("MK2"), R("R256"), C("l"), A.not_equal, 9984.0, A.mult)
+            ts(R("RST"), R("R256"), 0.0, A.is_gt)
+            ts(R("I16"), R("I16"), C("l"), A.add)
+            ts(R("TB"), R("I16"), float(TR), A.add)
         else:
             cp((("USED", 0, TR + 256), R("UO2")), R("ONE256"))
         tt(C("Tn"), C("Told"), C("e%d" % t), A.add)
@@ -446,21 +480,22 @@ def rank_program(g, core, T, topo):
         ts(R("BBI"), R("KBI"), 2, A.arith_shift_right, 4095, A.bitwise_and)
         tt(R("UO"), R("BBI"), R("NV"), A.add)
         tt(R("BC"), R("BBI"), R("NV"), A.add)
-        act(R("UG"), (("USED", 0, TR + 256), R("UO")), F.Copy)
+        act(R("UG"), (("USED", 0, TR + 256), R("UO")))
         mm([("P3", 0, 256, R("BO"), R("UG"), True, False)])
         for c in range(16):
             o = 256 * c + 16 * c
             ts(("E", o, 256 * c + 256), ("BR", 16 * c, 256), ("BC", c, c + 1), A.is_equal)
-            lst = [("P3", 16 * c, 16 * c + 16, R("SU"), ("E", o, o + 16), False, c == 15)]
+            act(("ED", 16 * c, 16 * c + 16), ("E", o, o + 16))
             if c < 15:
-                lst.append(("P3", 16 * c + 16, 256, R("BO"), ("E", o + 16, 256 * c + 256), False, False))
-            mm(lst)
+                mm([("P3", 16 * c + 16, 256, R("BO"), ("E", o + 16, 256 * c + 256), False, False)])
+        mm([("P3", 0, 256, R("SU"), R("ED"), False, True)])
         tt(R("XP"), ("P3", 0, 256), R("MK2"), A.is_gt)
         scan(R("XS"), R("RST"), R("XP"), 0.0, A.mult, A.add)
         xs = ("XS", 15, 256, 16)
-        scan(R("SK"), xs, xs, 0.0, A.add, A.max)
-        mm([("P4", 0, 16, R("NBO"), R("SK"), True, False), ("P4", 0, 16, R("UP"), xs, False, True),
-            ("P4", 16, 17, R("NBO"), ("SK", 15, 16), True, True)])
+        sk = ("I1", 0, 16)
+        scan(sk, xs, xs, 0.0, A.add, A.max)
+        mm([("P4", 0, 16, R("NBO"), sk, True, False), ("P4", 0, 16, R("UP"), xs, False, True),
+            ("P4", 16, 17, R("NBO"), ("I1", 15, 16), True, True)])
         tt(R("NK"), xs, R("TB"), A.mult)
         tt(R("PO"), ("P4", 0, 16), R("TI"), A.add)
         tt(R("SO"), R("PO"), R("NK"), A.max)

@@ -18,19 +18,19 @@ def _sb(dtype, **kw):
 
 
 _sb("bfloat16", BANK=TR + 256, CAND=J + DUM, TX=J, TY=J, TZ=J, USED=TR + 256, ONE256=256, FM=1024, SC=1024, I1=256, I2=256,
-    UG=256, E=4096, ED=256, XP=256, XS=256, SEND0=256, SEND1=256, SEND2=256, LAND0=256, LAND1=256, LAND2=256, BO=128, BO16=128,
-    BO256=128, NBO=128, IDN=128, NID=128, ID4=128, UP=128, NU=128, SU=128, WB=128, LS=2048, WKF=2048, WT=16, KP=256, MK2=256, RST=256,
+    UG=256, E=2048, XP=256, XS=272, SEND0=256, SEND1=256, SEND2=256, LAND0=256, LAND1=256, LAND2=256, BO=128, BO16=128,
+    BO256=128, NBO=128, IDN=128, NID=128, ID4=128, UP=128, NU=128, SU=128, WB=128, LS=2048, WKF=2048, WT=16, KP=256, MK2=256,
     rowg=128, rowl=128, rowk=128, rowh=128, R256=256, sB=64, IOC=258, JLC=128, AL=258, GM=128, LT=1024, X1=256, X2=256, OB=256)
-_sb("float32", sR=256, IC0=256, cols=64, RN=8, ra8=8, AS=8, M0=8, M1=8, AA=8, AB=8, T8=8, PRE=16, HL=16, DD=16, I16=16, TB=16,
-    TI=16, NK=16, C16=16, C256=16, W1T=64, W2S=72, W3S=1040, PK1=256, PK2=256, PK3=256, SEL8=128, NF=8, LX=256, LOT=128, HIT=128,
-    TRI=128, TRIS=128, ONE=128, ONES=128, rk6=128, F1=128, F1b=128, ZT=256, XT=256, YT=256, BC=16, NV=16, PO=16)
+_sb("float32", sR=256, IC0=256, cols=64, RN=8, ra8=8, AS=8, M0=8, M1=8, AA=8, AB=8, T8=32, T9=32, PRE=16, HL=16, DD=16, I16=16, TB=16,
+    TI=16, NK=16, C16=16, C256=16, W1T=64, W2S=72, W3S=1040, PK1=256, SEL8=128, NF=8, LX=256, LOT=128, HIT=128,
+    TRI=128, TRIS=128, ONE=128, ONES=128, rk6=128, F1=128, F1b=128, ZT=256, RCF=256, XT=256, YT=256, BC=16, NV=16, PO=16)
 _sb("int32", RA=768, RB=768, RC=768, ip=8, NI=8, WI=4, KI=256, OW=256, KRI=256, BRI=256, KBI=16, BBI=16)
 _sb("uint16", XO=256, YO=256, ZO=256, O1=16, O2=16, O3=16, UO=16, SO=16, UO2=16, BR=256)
 SCRATCH["UD"] = ("dram", [8, 4096], "bfloat16")
 for _b in range(8):
     SCRATCH["P%d" % _b] = ("psum", [128, 512], "float32")
 
-SEMAPHORES = ["cV", "cS", "cP", "cG"] + ["d%d" % i for i in range(12)] + ["arr0", "arr1", "arr2", "snt0", "snt1", "snt2"]
+SEMAPHORES = ["cV", "cS", "cP", "cG"] + ["d%d" % i for i in range(12)] + ["dU", "arr0", "arr1", "arr2", "snt0", "snt1", "snt2"]
 
 
 def rank_program(g, core, T, topo):
@@ -144,8 +144,8 @@ def rank_program(g, core, T, topo):
     def fill(r, c):
         do("V", lambda: g.vector.memset(ap(r), c), [], regs(r))
 
-    def act(out, in0, func=F.Copy, scale=1.0):
-        do("S", lambda: g.scalar.activation(ap(out), view(in0), func, bias=0.0, scale=view(scale)), regs(in0, scale), regs(out))
+    def act(out, in0, func=F.Copy, scale=1.0, acc=None):
+        do("S", lambda: g.scalar.activation(ap(out), view(in0), func, bias=0.0, scale=view(scale), accum_out=view(acc)), regs(in0, scale), regs(out, acc))
 
     def lin(out, in0, scale, bias):
         do("S", lambda: g.scalar.activation(ap(out), view(in0), F.Identity, bias=view(bias), scale=view(scale)), regs(in0, scale, bias), regs(out))
@@ -168,18 +168,20 @@ def rank_program(g, core, T, topo):
         return ("cols", names[name], names[name] + 1)
 
     def lists_z(t):
-        if t:
-            ts(C("Tq"), C("Told"), C("e%d" % t), A.add, 2.0 ** -12, A.mult)
-        ts(R("ZT"), R("RC", 256 * t, 256 * t + 256), C("Tq") if t else B / 4096.0, A.mult, -1920.5 + EPS, A.add)
+        if t == 0:
+            ts(R("ZT"), R("RC", 0, 256), B / 4096.0, A.mult, -1920.5 + EPS, A.add)
         ts(R("ZO"), R("ZT"), M23 + 1920.0, A.add, M23, A.subtract)
 
     dma("Y", T.NI[0:8, 0:4], T.ncl[:, :], [], [("NI", 0, 4)])
     dma("S", T.NI[0:8, 4:6], T.lim[:, :], [], [("NI", 4, 6)])
-    dma("Y", T.RC[:, 0:768], T.rc[:, :], [], [R("RC")])
+    dma("Y", T.RC[:, 0:256], T.rc[:, 0:256], [], [R("RC", 0, 256)])
     dma("S", T.BANK[:, 0:B], T.bank[:, :], [], [("BANK", 0, B)])
-    dma("Y", T.RA[:, 0:768], T.ra[:, :], [], [R("RA")])
-    dma("Y", T.RB[:, 0:768], T.rb[:, :], [], [R("RB")])
+    dma("Y", T.RA[:, 0:256], T.ra[:, 0:256], [], [R("RA", 0, 256)])
+    dma("Y", T.RB[:, 0:256], T.rb[:, 0:256], [], [R("RB", 0, 256)])
     dma("Y", T.KRI[:, 0:256], T.used[:, :], [], [R("KRI")])
+    dma("Y", T.RC[:, 256:768], T.rc[:, 256:768], [], [R("RC", 256)])
+    dma("Y", T.RA[:, 256:768], T.ra[:, 256:768], [], [R("RA", 256)])
+    dma("Y", T.RB[:, 256:768], T.rb[:, 256:768], [], [R("RB", 256)])
 
     ip = ("ip", 0, 1)
     iota(ip, [[0, 1]], 0, 1)
@@ -205,6 +207,7 @@ def rank_program(g, core, T, topo):
     iota(R("C256"), [[256, 4], [0, 4]])
     iota(R("I16"), [[16, 16]])
     iota(R("ONE256"), [[0, 256]], 1)
+    iota(("XS", 0, 16), [[0, 16]])
     iota(R("USED", TR, TR + 256), [[0, 256]], 1)
 
     ts(("ip", 1, 2), ip, 15, A.bitwise_and)
@@ -217,8 +220,6 @@ def rank_program(g, core, T, topo):
     cp(("cols", 0, 6), ("ip", 0, 6))
     ts(R("BO"), R("rowg"), C("g"), A.is_equal)
     ts(R("SEL8"), R("SEL8"), C("p"), A.is_equal)
-    do("V", lambda: g.vector.tensor_copy(T.NF[0:8, 0:6], T.NI[0:8, 0:6]), [("NI", 0, 6)], [("NF", 0, 6)])
-    mm([("P0", 8, 14, ("SEL8", 0, 128), ("NF", 0, 6, 1, 8), True, True)])
     lin(C("h0"), C("h"), -1.0, 1.0)
     act(R("BO256"), R("BO"), scale=256.0)
     lin(C("sg16"), C("h"), 0.125, -0.0625)
@@ -235,38 +236,65 @@ def rank_program(g, core, T, topo):
     ts(R("AS"), R("ra8"), C("kk"), A.add)
     m0 = ("M0", 0, 1)
     tt(C("m01"), m0, ("M0", 1, 2), A.subtract)
+    lin(C("zc"), C("h"), 0.0, -1920.5 + EPS)
     act(C("c7"), ("M0", 7, 8), scale=C("h0"))
     act(C("c6"), ("M0", 6, 7), scale=C("h0"))
     act(C("chi"), C("c7"), scale=-1920.0)
     act(C("c6"), C("c6"), scale=EPS)
     lin(C("clo"), C("c7"), -0.5, C("c6"))
     fill(R("RN"), 0.0)
-    act(("RN", 0, 3), ("P0", 8, 11))
-    act(C("e0"), ("P0", 11, 12))
-    lin(C("Told"), C("e0"), -1.0, float(B))
-    lists_z(0)
     tt(R("TRIS"), R("TRI"), R("rowh"), A.mult)
     tt(R("ONES"), R("ONE"), R("rowh"), A.mult)
     tt(R("F1"), R("F1b"), R("BO"), A.mult)
     lin(R("JLC"), R("F1"), 1.0, -1024.0)
+    do("V", lambda: g.vector.tensor_copy(T.NF[0:8, 0:6], T.NI[0:8, 0:6]), [("NI", 0, 6)], [("NF", 0, 6)])
+    mm([("P0", 8, 14, ("SEL8", 0, 128), ("NF", 0, 6, 1, 8), True, True)])
+    for i in (4, 5):
+        li, o = ("LX", 128 * (i - 4), 128 * (i - 4) + 128), 128 * (i - 3)
+        do("S", lambda: g.scalar.activation(T.LX[0:8, li[1]:li[2]], T.SEL8[0:8, 0:128], F.Identity, bias=T.NF[0:8, i:i + 1], scale=0.0),
+           [R("SEL8"), ("NF", i, i + 1)], [li])
+        mm([("P6", o, o + 128, li, ("SEL8", 0, 128, 1, 8), True, True)])
+    act(("RN", 0, 3), ("P0", 8, 11))
+    act(C("e0"), ("P0", 11, 12))
+    lin(C("Told"), C("e0"), -1.0, float(B))
+    act(R("LOT"), ("P6", 128, 256))
+    act(R("HIT"), ("P6", 256, 384))
+    lists_z(0)
+
+    def anti(t):
+        ts(R("AA"), R("AS"), float(3 + t), A.is_equal)
+        ts(R("AB"), R("AS"), float(4 + t), A.is_equal)
 
     def prepare(t):
-        s = 4 + t
-        ts(R("AA"), R("AS"), float(s - 1), A.is_equal)
-        ts(R("AB"), R("AS"), float(s), A.is_equal)
-        for m, c in (("M0", "PNL"), ("AA", "PNR"), ("M1", "dS"), ("AB", "Qc")):
-            tt(R("T8"), R("RN"), R(m), A.mult)
-            red(C(c), R("T8"))
-        tt(("PRE", 0, 1), C("PNL"), C("dS"), A.subtract)
-        tt(("PRE", 1, 2), C("PNR"), C("Qc"), A.subtract)
-        ts(C("dSb"), m0, C("Told"), A.mult, C("PNR"), A.subtract)
+        for i, (m, c) in enumerate((("M0", "PNL"), ("AA", "PNR"), ("M1", "dS"), ("AB", "Qc"))):
+            tt(R("T8", 8 * i, 8 * i + 8), R("RN"), R(m), A.mult)
+            act(R("T9", 8 * i, 8 * i + 8), R("T8", 8 * i, 8 * i + 8), acc=C(c))
+        lin(C("ml"), ("M0", 3 + t, 4 + t), 1.0, m0)
+        act(C("mc"), C("ml"), scale=16.0)
+
+    def prepare2(t):
+        lin(("PRE", 0, 1), C("dS"), -1.0, C("PNL"))
+        lin(("PRE", 1, 2), C("Qc"), -1.0, C("PNR"))
+        act(C("tm"), m0, scale=C("Told"))
+        lin(C("dSb"), C("PNR"), -1.0, C("tm"))
         for c, i in (("dS", 2), ("dSb", 6)):
             hi, lo = ("HL", i, i + 1), ("HL", i + 1, i + 2)
+            if t == 0 and i == 6:
+                ts(hi, C(c), M27, A.add, M27, A.subtract)
+                tt(lo, C(c), hi, A.subtract)
+                tt(hi, hi, C("chi"), A.add)
+                tt(lo, lo, C("clo"), A.add)
+                continue
             lin(lo, C(c), 1.0, M27)
             lin(hi, lo, 1.0, -M27)
             lin(lo, hi, -1.0, C(c))
             lin(lo, lo, 1.0, C("clo"))
             lin(hi, hi, 1.0, C("chi"))
+
+    def shares(t):
+        tt(("WI", 0, 1), C("PNL"), C("PNR"), A.mult)
+        ts(("WI", 1, 2), ("WI", 0, 1), 12, A.arith_shift_right)
+        ts(C("Wp"), ("WI", 1, 2), 16.0, A.mult)
 
     def newest(t):
         e = C("e%d" % t)
@@ -277,15 +305,35 @@ def rank_program(g, core, T, topo):
         for i in range(2):
             lin(("DD", 4 + i, 5 + i), ("DD", 2 + i, 3 + i), -1.0, ("DD", i, i + 1))
 
-    def decode_xy(t):
-        e, ml = C("e%d" % t), ("M0", 3 + t, 4 + t)
-        ts(C("NL"), ml, e, A.mult, C("PNL"), A.add)
-        ts(C("NR"), m0, e, A.mult, C("PNR"), A.add)
-        tt(("WI", 0, 1), C("NL"), C("NR"), A.mult)
-        ts(("WI", 1, 2), ("WI", 0, 1), 12, A.arith_shift_right)
-        ts(C("w"), ("WI", 1, 2), 16.0, A.mult)
+    def gath(o, c0, c1):
+        return (("BANK", 0, TR), (o, c0 // 16, c1 // 16))
+
+    def sg(b, o, c, n):
+        act(R(b, c, c + n), gath(o, c, c + n))
+
+    def decode(t):
+        if t == 0:
+            ts(("WI", 2, 3), C("e0"), ("RN", 0, 1), A.mult)
+        else:
+            ts(("WI", 2, 3), ("P4", 16, 17), 256.0, A.add, ("RN", 0, 1), A.mult)
+            lin(C("e%d" % t), ("P4", 16, 17), 1.0, 256.0)
+            lin(C("Tq"), C("e%d" % t), 2.0 ** -12, C("TqO"))
+            lin(R("ZT"), R("RCF"), C("Tq"), C("zc"))
+        ts(("WI", 3, 4), ("WI", 2, 3), 12, A.arith_shift_right)
+        ts(C("w"), ("WI", 3, 4), C("mc"), A.mult, C("Wp"), A.add)
         mm([("P0", 0, 1, R("TRI"), C("w"), True, True), ("P0", 1, 2, R("ONE"), C("w"), True, True)])
         mm([("P7", 0, 1, R("TRIS"), C("w"), True, True), ("P7", 1, 2, R("ONES"), C("w"), True, True)])
+        if t:
+            newest(t)
+            cp((("BANK", 0, TR + 256), R("SO")), R("LAND%d" % (t - 1)))
+            lists_z(t)
+        else:
+            ts(("DD", 0, 1), ("M0", 3, 4), C("e0"), A.mult, ("PRE", 0, 1), A.add)
+            ts(("DD", 1, 2), C("m01"), C("e0"), A.mult, ("PRE", 1, 2), A.add)
+            ts(("DD", 2, 4), ("DD", 0, 2), M27, A.add, M27, A.subtract)
+            tt(("DD", 4, 6), ("DD", 0, 2), ("DD", 2, 4), A.subtract)
+        sg("TZ", "ZO", 0, 1024)
+        sg("TZ", "ZO", 3072, 512)
         ts(R("AL", 0, 257), R("IOC", 0, 257), ("P0", 1, 2), A.mult, ("P0", 0, 1), A.is_ge)
         red(C("cnt"), R("AL", 0, 257))
         ts(C("th"), C("cnt"), -256.0, A.add, ("P7", 1, 2), A.mult)
@@ -297,19 +345,13 @@ def rank_program(g, core, T, topo):
                 ts(lt, R("GM"), c, A.mult, 2.0 ** -12, A.mult)
             else:
                 ts(lt, R("GM"), c, A.mult)
-            if i % 4 == 3:
-                pb, al = ("P1" if i == 3 else "P2"), ("AL", 0, 256)
-                mm([(pb, 256 * (x // 2), 256 * (x // 2) + 256, ("LT", 128 * (i - 3 + x), 128 * (i - 2 + x)), al, x % 2 == 0, x % 2 == 1) for x in range(4)])
-        for pb, r, x, o in (("P1", "RA", "XT", "XO"), ("P2", "RB", "YT", "YO")):
-            tt(R(x), (pb, 0, 256), R(r, 256 * t, 256 * t + 256), A.mult)
-            tt(R(x), (pb, 256, 512), R(x), A.add)
+            if i % 2:
+                pb, al = ("P1", "P3", "P2", "P4")[i // 2], ("AL", 0, 256)
+                mm([(pb, 0, 256, ("LT", 128 * (i - 1), 128 * i), al, True, False), (pb, 0, 256, lt, al, False, True)])
+        for pn, ps, r, x, o in (("P1", "P3", "RA", "XT", "XO"), ("P2", "P4", "RB", "YT", "YO")):
+            tt(R(x), (pn, 0, 256), R(r, 256 * t, 256 * t + 256), A.mult)
+            tt(R(x), (ps, 0, 256), R(x), A.add)
             ts(R(o), R(x), M23 + 1920.0, A.add, M23, A.subtract)
-
-    def gath(o, c0, c1):
-        return (("BANK", 0, TR), (o, c0 // 16, c1 // 16))
-
-    def sg(b, o, c, n):
-        act(R(b, c, c + n), gath(o, c, c + n))
 
     def add2(pb, c, n, w):
         mm([(pb, 0, n, R("IDN"), ("TX", c, c + n), True, False), (pb, 0, n, R(w), ("TY", c, c + n), False, True)])
@@ -335,34 +377,30 @@ def rank_program(g, core, T, topo):
         for p, f in enumerate(part(h)):
             ts(("FM",) + f, ("P%d" % (3 + h), 0, 128), float(p), A.is_equal)
 
-    def scans(h):
-        for f in part(h):
+    def scans(h, ps):
+        for f in [part(h)[p] for p in ps]:
             scan(("SC",) + f, ("FM",) + f, ("FM",) + f, ("SC", f[0] - 1, f[0]) if h else 0.0, A.add, A.max)
 
-    def counts(h):
-        for p in range(N):
-            pb, o, c = "P%d" % (5 + p // 2), 256 * (p % 2) + 128 * h, 256 * p + 128 * h
+    def counts(h, ps):
+        q = [("P%d" % (5 + p // 2), 256 * (p % 2) + 128 * h, 256 * p + 128 * h) for p in ps]
+        for pb, o, c in q:
             mm([(pb, o, o + 128, R("BO"), ("SC", c, c + 128), True, False), (pb, o, o + 128, R("NU"), ("FM", c, c + 128), False, True)])
-        for p in range(N):
-            pb, o, c = "P%d" % (5 + p // 2), 256 * (p % 2) + 128 * h, 256 * p + 128 * h
+        for pb, o, c in q:
             act(R("W3S", c, c + 128), (pb, o, o + 128))
 
     for t in range(RO):
         land, send = "LAND%d" % t, "SEND%d" % t
-        if t:
-            lists_z(t)
-            newest(t)
-        sg("TZ", "ZO", 0, 1024)
         if t == 0:
+            anti(0)
             prepare(0)
-            newest(0)
-        sg("TZ", "ZO", 3072, 1024)
-        decode_xy(t)
+            prepare2(0)
+            shares(0)
+        decode(t)
         if t == 0:
             cp(R("UG"), R("KRI"))
             dma("Y", T.UD[:, :], T.UG[:, 0:256], [R("UG")], [("UD", 0, 4096)])
             for l in range(16):
-                dma("Y", T.USED[l::16, 0:Q], T.UD[:, :], [("UD", 0, 4096)], [("USED", 0, Q)] if l == 15 else [], "d11")
+                dma("Y", T.USED[l::16, 0:Q], T.UD[:, :], [("UD", 0, 4096)], [("USED", 0, Q)] if l == 15 else [], "dU")
             act(R("NID"), R("IDN"), scale=-1.0)
         sg("TX", "XO", 1024, 1024)
         tt(R("TX", 0, 1024), gath("XO", 0, 1024), R("TZ", 0, 1024), A.min)
@@ -389,12 +427,7 @@ def rank_program(g, core, T, topo):
             sg("TY", "YO", c, 256)
         if t == 0:
             act(R("ID4"), R("IDN"), scale=4.0)
-            for i, b in ((4, "LOT"), (5, "HIT")):
-                li, o = ("LX", 128 * (i - 4), 128 * (i - 4) + 128), 128 * (i - 3)
-                do("V", lambda: g.vector.tensor_scalar(T.LX[0:8, li[1]:li[2]], T.SEL8[0:8, 0:128], 0.0, T.NF[0:8, i:i + 1], A.mult, A.add),
-                   [R("SEL8"), ("NF", i, i + 1)], [li])
-                mm([("P0", o, o + 128, li, ("SEL8", 0, 128, 1, 8), True, True)])
-                act(R(b), ("P0", o, o + 128))
+        sg("TZ", "ZO", 3584, 512)
         for c, n, pb in ((3072, 512, "P7"), (3584, 256, "P5"), (3840, 256, "P6")):
             add2(pb, c, n, "IDN")
             if c == 3072:
@@ -410,11 +443,12 @@ def rank_program(g, core, T, topo):
                 act(("LS", 128 * l + l, 128 * l + 128, 16), ("BO", 0, 128, 16))
             ts(R("KP"), R("R256"), C("l"), A.is_equal, 32768.0, A.mult)
         masks(0)
+        scans(0, (0, 1))
         codes(1)
-        scans(0)
-        counts(0)
+        scans(0, (2, 3))
+        counts(0, range(N))
         masks(1)
-        scans(1)
+        scans(1, range(N))
         mm([("P0", 64, 128, R("BO"), ("SC", 15, 1024, 16), True, True)])
         mm([("P7", 0, 64, ("LS", 128 * b, 128 * b + 128), ("SC", b, 1024, 16), b == 0, False) for b in range(11)])
         scan(R("W1T"), R("KP", 0, 64), ("P0", 64, 128), 0.0, A.max, A.min)
@@ -424,11 +458,14 @@ def rank_program(g, core, T, topo):
         mm([("P7", 0, 64, ("LS", 128 * b, 128 * b + 128), ("SC", b, 1024, 16), False, b == 15) for b in range(11, 16)])
         act(R("W2S", 0, 64), ("P7", 0, 64))
         mm([("P2", 0, 256, R("BO16"), R("I1"), True, False)])
-        counts(1)
+        counts(1, (0, 1))
+        if t < RO - 1:
+            anti(t + 1)
         scan(R("PK1"), R("KP"), ("P1", 0, 256), 0.0, A.max, A.min)
         tt(R("O1"), ("PK1", 15, 256, 16), R("C16"), A.add)
         tt(R("I2"), (("W2S", 0, 72), R("O1")), R("sR"), A.is_le)
         mm([("P2", 0, 256, R("BO"), R("I2"), False, True)])
+        counts(1, (2, 3))
         mm([("P3", 0, 256, R("BO256"), R("I1"), True, False)])
         mm([("P3", 0, 256, R("BO16"), R("I2"), False, False)])
         if t == 0:
@@ -436,16 +473,18 @@ def rank_program(g, core, T, topo):
             act(R("WB"), R("BO"), scale=C("wi"))
             act(R("WKF"), R("LS"), scale=C("wi"))
             act(R("NBO"), R("BO"), scale=-1.0)
-        scan(R("PK2"), R("KP"), ("P2", 0, 256), 0.0, A.max, A.min)
-        tt(R("O2"), ("PK2", 15, 256, 16), R("C256"), A.add)
+        if t < RO - 1:
+            cp(R("RCF"), R("RC", 256 * (t + 1), 256 * (t + 1) + 256))
+        scan(R("PK1"), R("KP"), ("P2", 0, 256), 0.0, A.max, A.min)
+        tt(R("O2"), ("PK1", 15, 256, 16), R("C256"), A.add)
         tt(R("XP"), (("W3S", 0, 1040), R("O2")), R("sR"), A.is_le)
         mm([("P3", 0, 256, R("BO"), R("XP"), False, True)])
-        scan(R("PK3"), R("KP"), ("P3", 0, 256), 0.0, A.max, A.min)
-        cp(R("O3"), ("PK3", 15, 256, 16))
+        scan(R("PK1"), R("KP"), ("P3", 0, 256), 0.0, A.max, A.min)
+        cp(R("O3"), ("PK1", 15, 256, 16))
         cp(R(send), (("CAND", 0, J + DUM), R("O3")))
         deps("G", [R(send)], [])
         tr, lo = [], 0
-        for d, ne in ((1, 4), (2, 4), (3, 8)):
+        for d, ne in ((1, 4), (2, 4), (3, 4)):
             p = (rank + d) % N
             rid, pid = topo.addr(T.cores[p])[:2]
             mask = sum(1 << x for x in topo.engines(core, T.cores[p])[lo:lo + ne])
@@ -453,23 +492,24 @@ def rank_program(g, core, T, topo):
             tr.append(RemoteDMATransfer(dst_ids=[DstId(rid=rid, pnc=pid)], dma_engine_mask=mask, remote_sem=T.sem["arr%d" % t],
                                         src=T[send][:, 64 * p:64 * p + 64], dst=T[land][:, 64 * rank:64 * rank + 64]))
         g.remote_dma_fused(tr, local_sem=T.sem["snt%d" % t])
-        count["snt%d" % t] = 16
-        count["arr%d" % t] = 16
-        note("G", [], [(land, 64 * p, 64 * p + 64) for p in range(N) if p != rank], ("arr%d" % t, 16), True)
-        cp((land, 64 * rank, 64 * rank + 64), (send, 64 * rank, 64 * rank + 64))
+        count["snt%d" % t] = 12
+        count["arr%d" % t] = 12
+        note("G", [], [(land, 64 * p, 64 * p + 64) for p in range(N) if p != rank], ("arr%d" % t, 12), True)
+        act((land, 64 * rank, 64 * rank + 64), (send, 64 * rank, 64 * rank + 64))
         if t == 0:
             ts(R("MK2"), R("R256"), C("l"), A.not_equal, 9984.0, A.mult)
-            ts(R("RST"), R("R256"), 0.0, A.is_gt)
             ts(R("I16"), R("I16"), C("l"), A.add)
             ts(R("TB"), R("I16"), float(TR), A.add)
         else:
+            tt(R("UO2"), R("BC"), R("NK"), A.max)
             cp((("USED", 0, TR + 256), R("UO2")), R("ONE256"))
-        tt(C("Tn"), C("Told"), C("e%d" % t), A.add)
-        cp(C("Told"), C("Tn"))
-        ts(R("TI"), R("I16"), C("Told"), A.add)
+        lin(C("Told"), C("Told"), 1.0, C("e%d" % t))
+        lin(R("TI"), R("I16"), 1.0, C("Told"))
         if t < RO - 1:
-            cp(("RN", 3 + t, 4 + t), C("e%d" % t))
+            act(("RN", 3 + t, 4 + t), C("e%d" % t))
             prepare(t + 1)
+            shares(t + 1)
+            act(C("TqO"), C("Told"), scale=2.0 ** -12)
         mm([("P1", 0, 256, R("WB"), R(land), True, True)])
         mm([("P2", 0, 16, ("WKF", 128 * l, 128 * l + 128), (land, l, 256, 16), l == 0, l == 15) for l in range(16)])
         cp(R("KRI"), ("P1", 0, 256))
@@ -478,32 +518,33 @@ def rank_program(g, core, T, topo):
         cp(R("KBI"), ("P2", 0, 16))
         ts(R("NV"), ("P2", 0, 16), 0.0, A.is_lt, 4096.0, A.mult)
         ts(R("BBI"), R("KBI"), 2, A.arith_shift_right, 4095, A.bitwise_and)
-        tt(R("UO"), R("BBI"), R("NV"), A.add)
         tt(R("BC"), R("BBI"), R("NV"), A.add)
+        cp(R("UO"), R("BC"))
         act(R("UG"), (("USED", 0, TR + 256), R("UO")))
-        mm([("P3", 0, 256, R("BO"), R("UG"), True, False)])
-        for c in range(16):
-            o = 256 * c + 16 * c
-            ts(("E", o, 256 * c + 256), ("BR", 16 * c, 256), ("BC", c, c + 1), A.is_equal)
-            act(("ED", 16 * c, 16 * c + 16), ("E", o, o + 16))
-            if c < 15:
-                mm([("P3", 16 * c + 16, 256, R("BO"), ("E", o + 16, 256 * c + 256), False, False)])
-        mm([("P3", 0, 256, R("SU"), R("ED"), False, True)])
+        if t < RO - 1:
+            prepare2(t + 1)
+        for n in range(16):
+            c = 4 * (n % 4) + n // 4
+            o = 512 * (c // 4) + 16 * (c % 4)
+            ts(("E", o, o + 256 - 16 * c), ("BR", 16 * c, 256), ("BC", c, c + 1), A.is_equal)
+            if c == 0:
+                mm([("P3", 0, 256, R("BO"), R("E", 0, 256), True, False), ("P3", 0, 16, R("NBO"), ("E", 0, 16), False, False)])
+            elif c < 15:
+                mm([("P3", 16 * c + 16, 256, R("BO"), ("E", o + 16, o + 256 - 16 * c), False, False)])
+            if n == 6:
+                mm([("P3", 0, 256, R("BO"), R("UG"), False, False)])
+        mm([("P3", 64 * k, 64 * k + 64, R("SU"), ("E", 512 * k, 512 * k + 64), False, k == 3) for k in range(4)])
         tt(R("XP"), ("P3", 0, 256), R("MK2"), A.is_gt)
-        scan(R("XS"), R("RST"), R("XP"), 0.0, A.mult, A.add)
-        xs = ("XS", 15, 256, 16)
-        sk = ("I1", 0, 16)
-        scan(sk, xs, xs, 0.0, A.add, A.max)
-        mm([("P4", 0, 16, R("NBO"), sk, True, False), ("P4", 0, 16, R("UP"), xs, False, True),
-            ("P4", 16, 17, R("NBO"), ("I1", 15, 16), True, True)])
-        tt(R("NK"), xs, R("TB"), A.mult)
+        scan(("XS", 16, 272), R("XP"), R("XP"), 0.0, A.add, A.max)
+        sk = ("XS", 31, 272, 16)
+        mm([("P4", 0, 16, R("NBO"), sk, True, False), ("P4", 0, 16, R("UP"), sk, False, False), ("P4", 1, 16, R("NU"), ("XS", 31, 256, 16), False, True),
+            ("P4", 16, 17, R("NBO"), ("XS", 271, 272), True, True)])
+        tt(R("NK"), sk, ("XS", 15, 256, 16), A.subtract)
+        tt(R("NK"), R("NK"), R("TB"), A.mult)
         tt(R("PO"), ("P4", 0, 16), R("TI"), A.add)
         tt(R("SO"), R("PO"), R("NK"), A.max)
-        cp((("BANK", 0, TR + 256), R("SO")), R(land))
-        if t < RO - 1:
-            ts(C("e%d" % (t + 1)), ("P4", 16, 17), 256.0, A.add)
-            tt(R("UO2"), R("BC"), R("NK"), A.max)
 
+    cp((("BANK", 0, TR + 256), R("SO")), R("LAND%d" % (RO - 1)))
     dma("Y", T.y[:, :], T.BANK[:, B:TR], [("BANK", B, TR)], [])
     for s in sorted(count):
         g.wait_ge(T.sem[s], count[s])

import numpy as np
from concourse.bass import DstId, RemoteDMATransfer
from concourse.mybir import dt, AluOpType as A, AxisListType, ActivationFunctionType as F

B, J, CAP, RO, Q, N = 3328, 4096, 64, 3, 4096, 4
TR = 4096
DUM = 288
M23 = 8388608.0
M27 = 201326592.0
EPS = 2.0 ** -13

SCRATCH = {}


def _sb(dtype, **kw):
    for n, w in kw.items():
        SCRATCH[n] = ("sbuf", [128, w], dtype)


_sb("bfloat16", BANK=TR + 256, CAND=J + DUM, TX=J, TY=J, TZ=J, USED=TR + 256, ONE256=256, FM=1024, SC=1024, I1=256, I2=256,
    UG=256, E=2048, XP=256, XS=272, SEND0=256, SEND1=256, SEND2=256, LAND0=256, LAND1=256, LAND2=256, BO=128, BO16=128,
    BO256=128, NBO=128, IDN=128, NID=128, ID4=128, UP=128, NU=128, SU=128, WB=128, LS=2048, WKF=2048, WT=16, KP=256, MK2=256,
    rowg=128, rowl=128, rowk=128, rowh=128, R256=256, sB=64, IOC=258, JLC=128, AL=258, GM=128, LT=1024, X1=256, X2=256, OB=256)
_sb("float32", sR=256, IC0=256, cols=64, RN=8, ra8=8, AS=8, M0=8, M1=8, AA=8, AB=8, T8=32, T9=32, PRE=16, HL=16, DD=16, I16=16, TB=16,
    TI=16, NK=16, C16=16, C256=16, W1T=64, W2S=72, W3S=1040, PK1=256, SEL8=128, NF=8, LX=256, LOT=128, HIT=128,
    TRI=128, TRIS=128, ONE=128, ONES=128, rk6=128, F1=128, F1b=128, ZT=256, RCF=256, XT=256, YT=256, BC=16, NV=16, PO=16)
_sb("int32", RA=768, RB=768, RC=768, ip=8, NI=8, WI=4, KI=256, OW=256, KRI=256, BRI=256, KBI=16, BBI=16)
_sb("uint16", XO=256, YO=256, ZO=256, O1=16, O2=16, O3=16, UO=16, SO=16, UO2=16, BR=256)
SCRATCH["UD"] = ("dram", [8, 4096], "bfloat16")
for _b in range(8):
    SCRATCH["P%d" % _b] = ("psum", [128, 512], "float32")

SEMAPHORES = ["cV", "cS", "cP", "cG"] + ["d%d" % i for i in range(12)] + ["dU", "arr0", "arr1", "arr2", "snt0", "snt1", "snt2"]


def rank_program(g, core, T, topo):
    rank = T.rank_of(core)
    if rank is None:
        return
    queue = {"V": g.vector, "S": g.scalar, "P": g.tensor, "G": g, "Y": g.sync}
    count, snap, recs, names, nd = {}, {}, {}, {}, [0]
    known = {q: {} for q in queue}

    def psum(b):
        return b[0] == "P" and b[1:].isdigit()

    def deps(q, reads, writes):
        need = {}
        for lst, w in ((reads, False), (writes, True)):
            for b, lo, hi in lst:
                for r in recs.get(b, []):
                    if psum(b):
                        if r[4] == q and (q == "P" or r[0] >= hi or r[1] <= lo or not (w or r[2])):
                            continue
                    elif r[0] >= hi or r[1] <= lo or not (w or r[2]):
                        continue
                    need[r[3][0]] = max(need.get(r[3][0], 0), r[3][1])
        for s, v in need.items():
            if known[q].get(s, 0) < v:
                queue[q].wait_ge(T.sem[s], v)
                known[q][s] = v
        for s, v in need.items():
            for s2, v2 in snap.get((s, v), {}).items():
                known[q][s2] = max(known[q].get(s2, 0), v2)

    def note(q, reads, writes, tok, remote=False):
        snap[tok] = {} if remote else dict(known[q])
        for b, lo, hi in writes:
            recs[b] = [r for r in recs.get(b, []) if not (r[0] >= lo and r[1] <= hi)] + [(lo, hi, True, tok, q)]
        for b, lo, hi in reads:
            keep = [r for r in recs.get(b, []) if r[2] or r[4] != q or not (r[0] >= lo and r[1] <= hi)]
            recs[b] = keep + [(lo, hi, False, tok, q)]

    def do(q, fn, reads, writes):
        deps(q, reads, writes)
        s = "c" + q
        count[s] = count.get(s, 0) + 1
        fn().then_inc(T.sem[s], 1)
        note(q, reads, writes, (s, count[s]))

    def mm(lst):
        reads = [x[3][:3] for x in lst] + [x[4][:3] for x in lst]
        writes = [x[:3] for x in lst]
        deps("P", reads, writes)
        last = None
        for x in lst:
            o, c0, c1, lh, rh, st, sp = x[:7]
            kp = rh[4] if len(rh) > 4 else 128
            lv = T[lh[0]][0:kp, lh[1]:lh[2]:lh[3] if len(lh) > 3 else 1]
            rv = T[rh[0]][0:kp, rh[1]:rh[2]:rh[3] if len(rh) > 3 else 1]
            last = g.tensor.matmul(T[o][:, c0:c1:x[7] if len(x) > 7 else 1], lv, rv, st, sp)
        count["cP"] = count.get("cP", 0) + 1
        last.then_inc(T.sem["cP"], 1)
        note("P", reads, writes, ("cP", count["cP"]))

    def dma(q, out, in_, reads, writes, sem=None):
        deps(q, reads, writes)
        if sem is None:
            sem = "d%d" % nd[0]
            nd[0] += 1
        queue[q].dma_start(out, in_).then_inc(T.sem[sem], 16)
        count[sem] = count.get(sem, 0) + 16
        note(q, reads, writes, (sem, count[sem]))

    def ap(r):
        return T[r[0]][:, r[1]:r[2]:r[3]] if len(r) > 3 else T[r[0]][:, r[1]:r[2]]

    def pair(x):
        return isinstance(x, tuple) and isinstance(x[0], tuple)

    def regs(*xs):
        out = []
        for x in xs:
            if pair(x):
                out += [x[0][:3], x[1][:3]]
            elif isinstance(x, tuple):
                out.append(x[:3])
        return out

    def view(x):
        return ap(x[0]).indirect(ap(x[1])) if pair(x) else ap(x) if isinstance(x, tuple) else x

    def ts(out, in0, s1, op0, s2=None, op1=None):
        if op1 is None:
            do("V", lambda: g.vector.tensor_scalar(ap(out), view(in0), view(s1), None, op0), regs(in0, s1), regs(out))
        else:
            do("V", lambda: g.vector.tensor_scalar(ap(out), view(in0), view(s1), view(s2), op0, op1), regs(in0, s1, s2), regs(out))

    def tt(out, in0, in1, op):
        do("V", lambda: g.vector.tensor_tensor(ap(out), view(in0), view(in1), op), regs(in0, in1), regs(out))

    def cp(out, in0):
        if pair(out):
            do("V", lambda: g.vector.tensor_copy(view(out), ap(in0)), regs(in0) + [out[1][:3]], [out[0][:3]])
        else:
            do("V", lambda: g.vector.tensor_copy(ap(out), view(in0)), regs(in0), regs(out))

    def scan(out, d0, d1, init, op0, op1):
        do("V", lambda: g.vector.tensor_tensor_scan(ap(out), ap(d0), ap(d1), view(init), op0, op1), regs(d0, d1, init), regs(out))

    def red(out, in0):
        do("V", lambda: g.vector.tensor_reduce(ap(out), ap(in0), AxisListType.X, A.add), regs(in0), regs(out))

    def fill(r, c):
        do("V", lambda: g.vector.memset(ap(r), c), [], regs(r))

    def act(out, in0, func=F.Copy, scale=1.0, acc=None):
        do("S", lambda: g.scalar.activation(ap(out), view(in0), func, bias=0.0, scale=view(scale), accum_out=view(acc)), regs(in0, scale), regs(out, acc))

    def lin(out, in0, scale, bias):
        do("S", lambda: g.scalar.activation(ap(out), view(in0), F.Identity, bias=view(bias), scale=view(scale)), regs(in0, scale, bias), regs(out))

    def iota(r, pattern, base=0, cm=0):
        if SCRATCH[r[0]][2] == "int32":
            do("G", lambda: g.iota(ap(r), pattern, base, cm), [], regs(r))
        else:
            do("G", lambda: g.iota(ap(r), pattern, base, cm, allow_small_or_imprecise_dtypes=True), [], regs(r))

    def sel(out, in0, pattern, op, fl, base, cm):
        do("G", lambda: g.affine_select(ap(out), ap(in0), pattern, op, fl, base, cm), regs(in0), regs(out))

    def R(b, lo=0, hi=None, *step):
        return (b, lo, SCRATCH[b][1][1] if hi is None else hi) + step

    def C(name):
        if name not in names:
            names[name] = len(names)
        return ("cols", names[name], names[name] + 1)

    def lists_z(t):
        if t == 0:
            ts(R("ZT"), R("RC", 0, 256), B / 4096.0, A.mult, -1920.5 + EPS, A.add)
        ts(R("ZO"), R("ZT"), M23 + 1920.0, A.add, M23, A.subtract)

    dma("Y", T.NI[0:8, 0:4], T.ncl[:, :], [], [("NI", 0, 4)])
    dma("S", T.NI[0:8, 4:6], T.lim[:, :], [], [("NI", 4, 6)])
    dma("Y", T.RC[:, 0:256], T.rc[:, 0:256], [], [R("RC", 0, 256)])
    dma("S", T.BANK[:, 0:B], T.bank[:, :], [], [("BANK", 0, B)])
    dma("Y", T.RA[:, 0:256], T.ra[:, 0:256], [], [R("RA", 0, 256)])
    dma("Y", T.RB[:, 0:256], T.rb[:, 0:256], [], [R("RB", 0, 256)])
    dma("Y", T.KRI[:, 0:256], T.used[:, :], [], [R("KRI")])
    dma("Y", T.RC[:, 256:768], T.rc[:, 256:768], [], [R("RC", 256)])
    dma("Y", T.RA[:, 256:768], T.ra[:, 256:768], [], [R("RA", 256)])
    dma("Y", T.RB[:, 256:768], T.rb[:, 256:768], [], [R("RB", 256)])

    ip = ("ip", 0, 1)
    iota(ip, [[0, 1]], 0, 1)
    iota(R("rowg"), [[1, 8], [0, 16]])
    iota(R("SEL8"), [[1, 8], [0, 16]])
    iota(R("rowk"), [[0, 16], [1, 8]])
    sel(R("rk6"), R("rowk"), [[0, 16], [-1, 8]], A.is_ge, -100.0, 5, 0)
    iota(R("ra8"), [[1, 8]])
    iota(R("rowl"), [[0, 8], [1, 16]])
    iota(R("rowh"), [[0, 8], [2, 2], [0, 8]], -1)
    iota(R("IC0"), [[1, 256]])
    iota(R("BANK", B, TR + 256), [[0, 1024]])
    iota(R("GM"), [[0, 128]], 1)
    sel(R("IDN"), R("GM"), [[-1, 128]], A.is_equal, 0.0, 0, 1)
    iota(R("R256"), [[0, 16], [1, 16]])
    iota(R("CAND", J, J + DUM), [[0, DUM]], -512)
    iota(R("W2S", 64, 72), [[0, 8]], 1000000)
    iota(R("W3S", 1024, 1040), [[0, 16]], 1000000)
    iota(R("LS"), [[0, 2048]])
    iota(R("sB"), [[1, 64]])
    iota(R("sR"), [[0, 4], [1, 64]])
    iota(R("C16"), [[16, 4], [0, 4]])
    iota(R("C256"), [[256, 4], [0, 4]])
    iota(R("I16"), [[16, 16]])
    iota(R("ONE256"), [[0, 256]], 1)
    iota(("XS", 0, 16), [[0, 16]])
    iota(R("USED", TR, TR + 256), [[0, 256]], 1)

    ts(("ip", 1, 2), ip, 15, A.bitwise_and)
    ts(("ip", 2, 3), ip, 7, A.bitwise_and)
    ts(("ip", 3, 4), ip, 3, A.logical_shift_right, 1, A.bitwise_and)
    ts(("ip", 4, 5), ip, 4, A.logical_shift_right)
    ts(("ip", 5, 6), ip, 1, A.bitwise_and)
    for c in "plkhgq":
        C(c)
    cp(("cols", 0, 6), ("ip", 0, 6))
    ts(R("BO"), R("rowg"), C("g"), A.is_equal)
    ts(R("SEL8"), R("SEL8"), C("p"), A.is_equal)
    lin(C("h0"), C("h"), -1.0, 1.0)
    act(R("BO256"), R("BO"), scale=256.0)
    lin(C("sg16"), C("h"), 0.125, -0.0625)
    ts(R("F1"), R("rk6"), C("k"), A.is_gt, C("h0"), A.mult)
    tt(R("TRI"), R("F1"), R("BO256"), A.mult)
    act(R("ONE"), R("BO"), scale=C("h0"))
    lin(R("F1b"), R("rowl"), C("sg16"), 1024.0)
    lin(R("IOC", 0, 256), R("IC0"), 1.0, C("h"))
    lin(R("IOC", 256, 257), C("h"), -256.0, 256.0)
    ts(R("M0"), R("ra8"), C("k"), A.is_equal)
    ts(R("M1"), R("ra8"), C("k"), A.subtract, -1.0, A.is_equal)
    ts(C("k6"), C("k"), 6.0, A.is_ge, 100.0, A.mult)
    tt(C("kk"), C("k"), C("k6"), A.add)
    ts(R("AS"), R("ra8"), C("kk"), A.add)
    m0 = ("M0", 0, 1)
    tt(C("m01"), m0, ("M0", 1, 2), A.subtract)
    lin(C("zc"), C("h"), 0.0, -1920.5 + EPS)
    act(C("c7"), ("M0", 7, 8), scale=C("h0"))
    act(C("c6"), ("M0", 6, 7), scale=C("h0"))
    act(C("chi"), C("c7"), scale=-1920.0)
    act(C("c6"), C("c6"), scale=EPS)
    lin(C("clo"), C("c7"), -0.5, C("c6"))
    fill(R("RN"), 0.0)
    tt(R("TRIS"), R("TRI"), R("rowh"), A.mult)
    tt(R("ONES"), R("ONE"), R("rowh"), A.mult)
    tt(R("F1"), R("F1b"), R("BO"), A.mult)
    lin(R("JLC"), R("F1"), 1.0, -1024.0)
    do("V", lambda: g.vector.tensor_copy(T.NF[0:8, 0:6], T.NI[0:8, 0:6]), [("NI", 0, 6)], [("NF", 0, 6)])
    mm([("P0", 8, 14, ("SEL8", 0, 128), ("NF", 0, 6, 1, 8), True, True)])
    for i in (4, 5):
        li, o = ("LX", 128 * (i - 4), 128 * (i - 4) + 128), 128 * (i - 3)
        do("S", lambda: g.scalar.activation(T.LX[0:8, li[1]:li[2]], T.SEL8[0:8, 0:128], F.Identity, bias=T.NF[0:8, i:i + 1], scale=0.0),
           [R("SEL8"), ("NF", i, i + 1)], [li])
        mm([("P6", o, o + 128, li, ("SEL8", 0, 128, 1, 8), True, True)])
    act(("RN", 0, 3), ("P0", 8, 11))
    act(C("e0"), ("P0", 11, 12))
    lin(C("Told"), C("e0"), -1.0, float(B))
    act(R("LOT"), ("P6", 128, 256))
    act(R("HIT"), ("P6", 256, 384))
    lists_z(0)

    def anti(t):
        ts(R("AA"), R("AS"), float(3 + t), A.is_equal)
        ts(R("AB"), R("AS"), float(4 + t), A.is_equal)

    def prepare(t):
        for i, (m, c) in enumerate((("M0", "PNL"), ("AA", "PNR"), ("M1", "dS"), ("AB", "Qc"))):
            tt(R("T8", 8 * i, 8 * i + 8), R("RN"), R(m), A.mult)
            act(R("T9", 8 * i, 8 * i + 8), R("T8", 8 * i, 8 * i + 8), acc=C(c))
        lin(C("ml"), ("M0", 3 + t, 4 + t), 1.0, m0)
        act(C("mc"), C("ml"), scale=16.0)

    def prepare2(t):
        lin(("PRE", 0, 1), C("dS"), -1.0, C("PNL"))
        lin(("PRE", 1, 2), C("Qc"), -1.0, C("PNR"))
        act(C("tm"), m0, scale=C("Told"))
        lin(C("dSb"), C("PNR"), -1.0, C("tm"))
        for c, i in (("dS", 2), ("dSb", 6)):
            hi, lo = ("HL", i, i + 1), ("HL", i + 1, i + 2)
            if t == 0 and i == 6:
                ts(hi, C(c), M27, A.add, M27, A.subtract)
                tt(lo, C(c), hi, A.subtract)
                tt(hi, hi, C("chi"), A.add)
                tt(lo, lo, C("clo"), A.add)
                continue
            lin(lo, C(c), 1.0, M27)
            lin(hi, lo, 1.0, -M27)
            lin(lo, hi, -1.0, C(c))
            lin(lo, lo, 1.0, C("clo"))
            lin(hi, hi, 1.0, C("chi"))

    def shares(t):
        tt(("WI", 0, 1), C("PNL"), C("PNR"), A.mult)
        ts(("WI", 1, 2), ("WI", 0, 1), 12, A.arith_shift_right)
        ts(C("Wp"), ("WI", 1, 2), 16.0, A.mult)

    def newest(t):
        e = C("e%d" % t)
        for i, m in enumerate((("M0", 3 + t, 4 + t), C("m01"))):
            lin(("DD", i, i + 1), m, e, ("PRE", i, i + 1))
        lin(("DD", 6, 8), ("DD", 0, 2), 1.0, M27)
        lin(("DD", 2, 4), ("DD", 6, 8), 1.0, -M27)
        for i in range(2):
            lin(("DD", 4 + i, 5 + i), ("DD", 2 + i, 3 + i), -1.0, ("DD", i, i + 1))

    def gath(o, c0, c1):
        return (("BANK", 0, TR), (o, c0 // 16, c1 // 16))

    def sg(b, o, c, n):
        act(R(b, c, c + n), gath(o, c, c + n))

    def decode(t):
        if t == 0:
            ts(("WI", 2, 3), C("e0"), ("RN", 0, 1), A.mult)
        else:
            ts(("WI", 2, 3), ("P4", 16, 17), 256.0, A.add, ("RN", 0, 1), A.mult)
            lin(C("e%d" % t), ("P4", 16, 17), 1.0, 256.0)
            lin(C("Tq"), C("e%d" % t), 2.0 ** -12, C("TqO"))
            lin(R("ZT"), R("RCF"), C("Tq"), C("zc"))
        ts(("WI", 3, 4), ("WI", 2, 3), 12, A.arith_shift_right)
        ts(C("w"), ("WI", 3, 4), C("mc"), A.mult, C("Wp"), A.add)
        mm([("P0", 0, 1, R("TRI"), C("w"), True, True), ("P0", 1, 2, R("ONE"), C("w"), True, True)])
        mm([("P7", 0, 1, R("TRIS"), C("w"), True, True), ("P7", 1, 2, R("ONES"), C("w"), True, True)])
        if t:
            newest(t)
            cp((("BANK", 0, TR + 256), R("SO")), R("LAND%d" % (t - 1)))
            lists_z(t)
        else:
            ts(("DD", 0, 1), ("M0", 3, 4), C("e0"), A.mult, ("PRE", 0, 1), A.add)
            ts(("DD", 1, 2), C("m01"), C("e0"), A.mult, ("PRE", 1, 2), A.add)
            ts(("DD", 2, 4), ("DD", 0, 2), M27, A.add, M27, A.subtract)
            tt(("DD", 4, 6), ("DD", 0, 2), ("DD", 2, 4), A.subtract)
        sg("TZ", "ZO", 0, 1024)
        sg("TZ", "ZO", 3072, 512)
        ts(R("AL", 0, 257), R("IOC", 0, 257), ("P0", 1, 2), A.mult, ("P0", 0, 1), A.is_ge)
        red(C("cnt"), R("AL", 0, 257))
        ts(C("th"), C("cnt"), -256.0, A.add, ("P7", 1, 2), A.mult)
        ts(C("th2"), C("th"), ("P7", 0, 1), A.add, C("h0"), A.add)
        ts(R("GM"), R("JLC"), ("P0", 1, 2), A.mult, C("th2"), A.is_ge)
        for i, c in enumerate((("DD", 2, 3), ("DD", 4, 5), ("HL", 2, 3), ("HL", 3, 4), ("DD", 3, 4), ("DD", 5, 6), ("HL", 6, 7), ("HL", 7, 8))):
            lt = ("LT", 128 * i, 128 * i + 128)
            if c[0] == "DD":
                ts(lt, R("GM"), c, A.mult, 2.0 ** -12, A.mult)
            else:
                ts(lt, R("GM"), c, A.mult)
            if i % 2:
                pb, al = ("P1", "P3", "P2", "P4")[i // 2], ("AL", 0, 256)
                mm([(pb, 0, 256, ("LT", 128 * (i - 1), 128 * i), al, True, False), (pb, 0, 256, lt, al, False, True)])
        for pn, ps, r, x, o in (("P1", "P3", "RA", "XT", "XO"), ("P2", "P4", "RB", "YT", "YO")):
            tt(R(x), (pn, 0, 256), R(r, 256 * t, 256 * t + 256), A.mult)
            tt(R(x), (ps, 0, 256), R(x), A.add)
            ts(R(o), R(x), M23 + 1920.0, A.add, M23, A.subtract)

    def add2(pb, c, n, w):
        mm([(pb, 0, n, R("IDN"), ("TX", c, c + n), True, False), (pb, 0, n, R(w), ("TY", c, c + n), False, True)])

    def sumkey(h):
        mm([("P%d" % (1 + h), l, 256, ("CAND", 2048 * h + l, 2048 * h + 2048, 16), R("WT"), True, True, 16) for l in range(16)])

    def codes(h):
        pb, a = "P%d" % (1 + h), (128 * h, 128 * h + 128)
        cp(R("KI", *a), (pb, 128, 256))
        tt(R("X1", *a), (pb, 0, 128), R("LOT"), A.is_lt)
        tt(R("X2", *a), (pb, 0, 128), R("HIT"), A.is_gt)
        ts(R("OW", *a), R("KI", *a), 3, A.bitwise_and)
        cp(R("OB", *a), R("OW", *a))
        pc = "P%d" % (3 + h)
        mm([(pc, 0, 128, R("X1", *a), R("ID4"), True, False), (pc, 0, 128, R("X2", *a), R("ID4"), False, False),
            (pc, 0, 128, R("OB", *a), R("IDN"), False, True)])

    def part(h):
        return [(256 * p + 128 * h, 256 * p + 128 * h + 128) for p in range(N)]

    def masks(h):
        for p, f in enumerate(part(h)):
            ts(("FM",) + f, ("P%d" % (3 + h), 0, 128), float(p), A.is_equal)

    def scans(h, ps):
        for f in [part(h)[p] for p in ps]:
            scan(("SC",) + f, ("FM",) + f, ("FM",) + f, ("SC", f[0] - 1, f[0]) if h else 0.0, A.add, A.max)

    def counts(h, ps):
        q = [("P%d" % (5 + p // 2), 256 * (p % 2) + 128 * h, 256 * p + 128 * h) for p in ps]
        for pb, o, c in q:
            mm([(pb, o, o + 128, R("BO"), ("SC", c, c + 128), True, False), (pb, o, o + 128, R("NU"), ("FM", c, c + 128), False, True)])
        for pb, o, c in q:
            act(R("W3S", c, c + 128), (pb, o, o + 128))

    for t in range(RO):
        land, send = "LAND%d" % t, "SEND%d" % t
        if t == 0:
            anti(0)
            prepare(0)
            prepare2(0)
            shares(0)
        decode(t)
        if t == 0:
            cp(R("UG"), R("KRI"))
            dma("Y", T.UD[:, :], T.UG[:, 0:256], [R("UG")], [("UD", 0, 4096)])
            for l in range(16):
                dma("Y", T.USED[l::16, 0:Q], T.UD[:, :], [("UD", 0, 4096)], [("USED", 0, Q)] if l == 15 else [], "dU")
            act(R("NID"), R("IDN"), scale=-1.0)
        sg("TX", "XO", 1024, 1024)
        tt(R("TX", 0, 1024), gath("XO", 0, 1024), R("TZ", 0, 1024), A.min)
        tt(R("CAND", 0, 1024), gath("YO", 0, 1024), R("TX", 0, 1024), A.min)
        for i in range(2):
            c = 2048 + 512 * i
            sg("TX", "XO", c, 512)
            sg("TY", "YO", c, 512)
            add2("P%d" % (5 + i), c, 512, "NID")
        sg("TX", "XO", 3072, 512)
        for i in range(2):
            act(R("TZ", 2048 + 512 * i, 2560 + 512 * i), ("P%d" % (5 + i), 0, 512), F.Abs)
        tt(R("TY", 1024, 2048), gath("YO", 1024, 2048), R("TX", 1024, 2048), A.max)
        tt(R("CAND", 1024, 2048), gath("ZO", 1024, 2048), R("TY", 1024, 2048), A.min)
        if t == 0:
            cp(R("WT", 0, 8), ("BO", 0, 128, 16))
            ts(C("s4"), C("q"), -2.0, A.mult, 1.0, A.add)
            ts(R("WT", 8, 16), R("WT", 0, 8), C("s4"), A.mult)
        sumkey(0)
        tt(R("CAND", 2048, 3072), gath("ZO", 2048, 3072), R("TZ", 2048, 3072), A.min)
        sg("TY", "YO", 3072, 512)
        for c in (3584, 3840):
            sg("TX", "XO", c, 256)
            sg("TY", "YO", c, 256)
        if t == 0:
            act(R("ID4"), R("IDN"), scale=4.0)
        sg("TZ", "ZO", 3584, 512)
        for c, n, pb in ((3072, 512, "P7"), (3584, 256, "P5"), (3840, 256, "P6")):
            add2(pb, c, n, "IDN")
            if c == 3072:
                codes(0)
            tt(R("CAND", c, c + n), (pb, 0, n), R("TZ", c, c + n), A.min)
        sumkey(1)
        if t == 0:
            sel(R("UP"), R("BO"), [[-1, 128]], A.is_gt, 0.0, 0, 1)
            sel(R("SU"), R("BO"), [[1, 128]], A.is_gt, 0.0, 0, -1)
            act(R("NU"), R("UP"), scale=-1.0)
            act(R("BO16"), R("BO"), scale=16.0)
            for l in range(16):
                act(("LS", 128 * l + l, 128 * l + 128, 16), ("BO", 0, 128, 16))
            ts(R("KP"), R("R256"), C("l"), A.is_equal, 32768.0, A.mult)
        masks(0)
        scans(0, (0, 1))
        codes(1)
        scans(0, (2, 3))
        counts(0, range(N))
        masks(1)
        scans(1, range(N))
        mm([("P0", 64, 128, R("BO"), ("SC", 15, 1024, 16), True, True)])
        mm([("P7", 0, 64, ("LS", 128 * b, 128 * b + 128), ("SC", b, 1024, 16), b == 0, False) for b in range(11)])
        scan(R("W1T"), R("KP", 0, 64), ("P0", 64, 128), 0.0, A.max, A.min)
        for p in range(N):
            ts(("I1", 64 * p, 64 * p + 64), R("sB"), ("W1T", 16 * p + 15, 16 * p + 16), A.is_ge)
        mm([("P1", 0, 256, R("BO"), R("I1"), True, True)])
        mm([("P7", 0, 64, ("LS", 128 * b, 128 * b + 128), ("SC", b, 1024, 16), False, b == 15) for b in range(11, 16)])
        act(R("W2S", 0, 64), ("P7", 0, 64))
        mm([("P2", 0, 256, R("BO16"), R("I1"), True, False)])
        counts(1, (0, 1))
        if t < RO - 1:
            anti(t + 1)
        scan(R("PK1"), R("KP"), ("P1", 0, 256), 0.0, A.max, A.min)
        tt(R("O1"), ("PK1", 15, 256, 16), R("C16"), A.add)
        tt(R("I2"), (("W2S", 0, 72), R("O1")), R("sR"), A.is_le)
        mm([("P2", 0, 256, R("BO"), R("I2"), False, True)])
        counts(1, (2, 3))
        mm([("P3", 0, 256, R("BO256"), R("I1"), True, False)])
        mm([("P3", 0, 256, R("BO16"), R("I2"), False, False)])
        if t == 0:
            ts(C("wi"), C("l"), 14.0, A.mult, 9.0, A.add)
            act(R("WB"), R("BO"), scale=C("wi"))
            act(R("WKF"), R("LS"), scale=C("wi"))
            act(R("NBO"), R("BO"), scale=-1.0)
        if t < RO - 1:
            cp(R("RCF"), R("RC", 256 * (t + 1), 256 * (t + 1) + 256))
        scan(R("PK1"), R("KP"), ("P2", 0, 256), 0.0, A.max, A.min)
        tt(R("O2"), ("PK1", 15, 256, 16), R("C256"), A.add)
        tt(R("XP"), (("W3S", 0, 1040), R("O2")), R("sR"), A.is_le)
        mm([("P3", 0, 256, R("BO"), R("XP"), False, True)])
        scan(R("PK1"), R("KP"), ("P3", 0, 256), 0.0, A.max, A.min)
        cp(R("O3"), ("PK1", 15, 256, 16))
        cp(R(send), (("CAND", 0, J + DUM), R("O3")))
        deps("G", [R(send)], [])
        tr, lo = [], 0
        for d, ne in ((1, 4), (2, 4), (3, 4)):
            p = (rank + d) % N
            rid, pid = topo.addr(T.cores[p])[:2]
            mask = sum(1 << x for x in topo.engines(core, T.cores[p])[lo:lo + ne])
            lo += ne
            tr.append(RemoteDMATransfer(dst_ids=[DstId(rid=rid, pnc=pid)], dma_engine_mask=mask, remote_sem=T.sem["arr%d" % t],
                                        src=T[send][:, 64 * p:64 * p + 64], dst=T[land][:, 64 * rank:64 * rank + 64]))
        g.remote_dma_fused(tr, local_sem=T.sem["snt%d" % t])
        count["snt%d" % t] = 12
        count["arr%d" % t] = 12
        note("G", [], [(land, 64 * p, 64 * p + 64) for p in range(N) if p != rank], ("arr%d" % t, 12), True)
        act((land, 64 * rank, 64 * rank + 64), (send, 64 * rank, 64 * rank + 64))
        if t == 0:
            ts(R("MK2"), R("R256"), C("l"), A.not_equal, 9984.0, A.mult)
            ts(R("I16"), R("I16"), C("l"), A.add)
            ts(R("TB"), R("I16"), float(TR), A.add)
        else:
            tt(R("UO2"), R("BC"), R("NK"), A.max)
            cp((("USED", 0, TR + 256), R("UO2")), R("ONE256"))
        lin(C("Told"), C("Told"), 1.0, C("e%d" % t))
        lin(R("TI"), R("I16"), 1.0, C("Told"))
        if t < RO - 1:
            act(("RN", 3 + t, 4 + t), C("e%d" % t))
            prepare(t + 1)
            shares(t + 1)
            act(C("TqO"), C("Told"), scale=2.0 ** -12)
        mm([("P1", 0, 256, R("WB"), R(land), True, True)])
        mm([("P2", 0, 16, ("WKF", 128 * l, 128 * l + 128), (land, l, 256, 16), l == 0, l == 15) for l in range(16)])
        cp(R("KRI"), ("P1", 0, 256))
        ts(R("BRI"), R("KRI"), 2, A.arith_shift_right, 4095, A.bitwise_and)
        cp(R("BR"), R("BRI"))
        cp(R("KBI"), ("P2", 0, 16))
        ts(R("NV"), ("P2", 0, 16), 0.0, A.is_lt, 4096.0, A.mult)
        ts(R("BBI"), R("KBI"), 2, A.arith_shift_right, 4095, A.bitwise_and)
        tt(R("BC"), R("BBI"), R("NV"), A.add)
        cp(R("UO"), R("BC"))
        act(R("UG"), (("USED", 0, TR + 256), R("UO")))
        if t < RO - 1:
            prepare2(t + 1)
        for n in range(16):
            c = 4 * (n % 4) + n // 4
            o = 512 * (c // 4) + 16 * (c % 4)
            ts(("E", o, o + 256 - 16 * c), ("BR", 16 * c, 256), ("BC", c, c + 1), A.is_equal)
            if c == 0:
                mm([("P3", 0, 256, R("BO"), R("E", 0, 256), True, False), ("P3", 0, 16, R("NBO"), ("E", 0, 16), False, False)])
            elif c < 15:
                mm([("P3", 16 * c + 16, 256, R("BO"), ("E", o + 16, o + 256 - 16 * c), False, False)])
            if n == 6:
                mm([("P3", 0, 256, R("BO"), R("UG"), False, False)])
        mm([("P3", 64 * k, 64 * k + 64, R("SU"), ("E", 512 * k, 512 * k + 64), False, k == 3) for k in range(4)])
        tt(R("XP"), ("P3", 0, 256), R("MK2"), A.is_gt)
        scan(("XS", 16, 272), R("XP"), R("XP"), 0.0, A.add, A.max)
        sk = ("XS", 31, 272, 16)
        mm([("P4", 0, 16, R("NBO"), sk, True, False), ("P4", 0, 16, R("UP"), sk, False, False), ("P4", 1, 16, R("NU"), ("XS", 31, 256, 16), False, True),
            ("P4", 16, 17, R("NBO"), ("XS", 271, 272), True, True)])
        tt(R("NK"), sk, ("XS", 15, 256, 16), A.subtract)
        tt(R("NK"), R("NK"), R("TB"), A.mult)
        tt(R("PO"), ("P4", 0, 16), R("TI"), A.add)
        tt(R("SO"), R("PO"), R("NK"), A.max)

    cp((("BANK", 0, TR + 256), R("SO")), R("LAND%d" % (RO - 1)))
    dma("Y", T.y[:, :], T.BANK[:, B:TR], [("BANK", B, TR)], [])
    for s in sorted(count):
        g.wait_ge(T.sem[s], count[s])
